import numpy as np
import ml_dtypes


def mxq(x, axis, fmt="e4m3"):
    dtype, down = {"e4m3": (ml_dtypes.float8_e4m3fn, 7), "e5m2": (ml_dtypes.float8_e5m2, 14)}[fmt]
    v = np.moveaxis(np.asarray(x, np.float32).astype(ml_dtypes.bfloat16).astype(np.float64), axis, -1)
    blocks = v.reshape(v.shape[:-1] + (-1, 32))
    amax = np.abs(blocks).max(-1, keepdims=True)
    byte = np.maximum(np.where(amax > 0, np.frexp(amax)[1] - 1 + 127, 0) - down, 1)
    scale = np.exp2(byte - 127.0)
    codes = (blocks / scale).astype(np.float32).astype(dtype).astype(np.float64)
    return np.moveaxis((codes * scale).reshape(v.shape), -1, axis)


WIDE = False


def mx_kscale(k):
    if not WIDE:
        return np.ones(k)
    levels = np.array([10, -10, 5, -5, 0])
    if k % 512:
        return np.exp2(np.random.permutation(np.resize(levels, k // 32))).repeat(32)
    a = np.empty((k // 512, 16))
    for p in range(k // 512):
        a[p, :8] = np.random.permutation(np.resize(levels, 8))
        for g in range(8):
            far = levels[np.abs(levels - a[p, g]) >= 10]
            a[p, g + 8] = far[np.random.randint(len(far))]
    return np.exp2(a.ravel()).repeat(32)


def f64(x):
    return np.asarray(x).astype(np.float64)


def striped(idx):
    return np.tile(idx.reshape(-1, 16).T, (8, 1)).astype(np.uint16)


def unstriped(offs):
    return offs[:16].T.reshape(-1).astype(np.int64)


E2M1 = np.array([0.0, 0.5, 1.0, 1.5, 2.0, 3.0, 4.0, 6.0, -0.0, -0.5, -1.0, -1.5, -2.0, -3.0, -4.0, -6.0])


def pack_weight(w, fmt):
    k, n = w.shape
    w = f64(np.asarray(w, np.float32).astype(ml_dtypes.bfloat16)).reshape(k // 32, 32, n)
    amax = np.abs(w).max(1)
    if fmt == "e4m3":
        byte = np.frexp(amax)[1] - 1 + 127 - 7
    else:
        mant, ex = np.frexp(amax / 6.0)
        byte = np.where(mant > 0.5, ex, ex - 1) + 127
    byte = np.clip(np.where(amax > 0, byte, 1), 1, 254)
    scaled = (w * np.exp2(127.0 - byte)[:, None, :]).reshape(k, n).astype(np.float32)
    by_word = np.ascontiguousarray(scaled.reshape(k // 512, 128, 4, n).transpose(0, 1, 3, 2))
    if fmt == "e4m3":
        words = by_word.astype(ml_dtypes.float8_e4m3fn).view(np.uint8)
    else:
        c = by_word.astype(ml_dtypes.float4_e2m1fn).view(np.uint8) & 0xF
        words = (c[..., 0::2] | (c[..., 1::2] << 4)).reshape(k // 512, 128, 2 * n)
    return np.ascontiguousarray(words), np.ascontiguousarray(byte.astype(np.uint8).reshape(k // 512, 16, n))


def unpack_weight(words, scales, fmt):
    g, _, n = scales.shape
    words = np.ascontiguousarray(words).reshape(g, 128, n, -1)
    if fmt == "e4m3":
        vals = words.view(ml_dtypes.float8_e4m3fn).astype(np.float64)
    else:
        nib = np.empty((g, 128, n, 4), np.uint8)
        nib[..., 0::2] = words & 0xF
        nib[..., 1::2] = words >> 4
        vals = E2M1[nib]
    vals = vals * np.repeat(np.exp2(scales.astype(np.float64) - 127.0), 8, axis=1)[..., None]
    return vals.transpose(0, 1, 3, 2).reshape(g * 512, n)


def gelu(v):
    return 0.5 * v * (1.0 + np.tanh(np.sqrt(2.0 / np.pi) * (v + 0.044715 * v**3)))


def bf(x):
    return np.asarray(x, np.float32).astype(ml_dtypes.bfloat16)


def planes(Y):
    n, m = Y.shape
    b = f64(bf(Y)).reshape(n // 32, 32, m)
    amax = np.abs(b).max(1)
    byte = np.clip(np.where(amax > 0, np.frexp(amax)[1] - 1 + 127 - 7, 1), 1, 254)
    codes = (b * np.exp2(127.0 - byte)[:, None, :]).reshape(n, m).astype(np.float32).astype(ml_dtypes.float8_e4m3fn).view(np.uint8)
    words = codes.reshape(n // 512, 128, 4, m).transpose(0, 1, 3, 2)
    return np.ascontiguousarray(words), np.ascontiguousarray(byte.astype(np.uint8).reshape(n // 512, 16, m))


K, K2, H, T, T3, S, T2, P = 1024, 512, 1024, 2048, 1024, 512, 2048, 1024

def setup_inputs():
    n = np.random.standard_normal
    s, s2, u = mx_kscale(K)[:, None], mx_kscale(K2)[:, None], mx_kscale(H)[:, None]
    gr = np.exp(0.8 * n(H))
    d = {}
    d["tab_words"], d["tab_scales"] = pack_weight(n((K, T)) * s, "e4m3")
    d["tab2_words"], d["tab2_scales"] = pack_weight(n((K2, T3)) * s2, "e4m3")
    d["offs"] = striped(np.random.permutation(T)[:S])
    d["offs2"] = striped(np.random.permutation(T3)[:S])
    perm = np.random.permutation(T2)
    d["offs3"], d["offs4"] = striped(perm[:S]), striped(perm[S:2 * S])
    d["offs5"] = striped(np.random.permutation(T2)[:P])
    d["wt"] = (n((K, H)) * 1.3 / K**0.5 / s).astype(np.float32)
    d["wv_words"], d["wv_scales"] = pack_weight(n((K, H)) * 1.5 / K**0.5 / s * u.T, "e2m1")
    d["wf_words"], d["wf_scales"] = pack_weight(n((K2, H)) / K2**0.5 / s2 * u.T, "e4m3")
    d["floors"] = (0.7 * n((H, S)) * u).astype(np.float32)
    d["wg1"] = np.exp(0.3 * n((128, S))).astype(np.float32)
    d["wg2"] = np.exp(0.3 * n((128, S))).astype(np.float32)
    d["page0"] = (n((H, T2)) * u).astype(np.float32)
    d["shift"] = (0.7 * n(H) * u[:, 0]).astype(np.float32)
    d["wo"] = (n((H, H)) * 0.8 / H**0.5 / u * gr).astype(np.float32)
    d["gy"] = (0.5 * gr / u[:, 0]).astype(np.float32)
    return d

def reference(tab_words, tab_scales, tab2_words, tab2_scales, offs, offs2, offs3, offs4, offs5,
              wt, wv_words, wv_scales, wf_words, wf_scales, floors, wg1, wg2, page0, shift, wo, gy):
    v = unpack_weight(tab_words, tab_scales, "e4m3")[:, unstriped(offs)]
    v2 = unpack_weight(tab2_words, tab2_scales, "e4m3")[:, unstriped(offs2)]
    wv = unpack_weight(wv_words, wv_scales, "e2m1")
    wf = unpack_weight(wf_words, wf_scales, "e4m3")
    snow = wv.T @ v
    h1 = np.tanh(mxq(f64(wt), 0, "e4m3").T @ v) * snow
    h2 = np.maximum(wf.T @ v2, f64(floors))
    page = f64(page0).copy()
    page[:, unstriped(offs3)] = np.tile(f64(wg1), (H // 128, 1)) * h1
    page[:, unstriped(offs4)] = np.tile(f64(wg2), (H // 128, 1)) * h2
    slots = page[:, unstriped(offs5)]
    x = mxq(slots + f64(shift)[:, None], 0, "e4m3")
    y = np.tanh(mxq(f64(wo), 0, "e4m3").T @ x) + f64(gy)[:, None] * slots
    words, scales = planes(y)
    return y, words, scales

@@ -1,0 +1,263 @@
+from contextlib import ExitStack
+
+import concourse.mybir as mybir
+
+K, K2, H, T, T3, S, T2, NP = 1024, 512, 1024, 2048, 1024, 512, 2048, 1024
+FLOPS = 2 * (2 * K * H * S + K2 * H * S + H * H * NP)
+
+F32 = mybir.dt.float32
+BF16 = mybir.dt.bfloat16
+I32 = mybir.dt.int32
+U32 = mybir.dt.uint32
+U16 = mybir.dt.uint16
+U8 = mybir.dt.uint8
+FP8X4 = mybir.dt.float8_e4m3fn_x4
+FP4X4 = mybir.dt.float4_e2m1fn_x4
+ACT = mybir.ActivationFunctionType
+ALU = mybir.AluOpType
+
+P = 128
+HALF = 512
+Y_VEC = 256
+
+
+def tile_list_glide_slab_page_kernel(
+    tc, tab_words, tab_scales, tab2_words, tab2_scales, offs, offs2, offs3, offs4, offs5,
+    wt, wv_words, wv_scales, wf_words, wf_scales, floors, wg1, wg2, page0, shift, wo, gy,
+    out_0, out_1, out_2,
+):
+    nc = tc.nc
+    with ExitStack() as ctx:
+        keep = ctx.enter_context(tc.tile_pool(name="keep", bufs=1))
+        ring = ctx.enter_context(tc.tile_pool(name="ring", bufs=1))
+        psum = ctx.enter_context(tc.psum_pool(name="psum", bufs=1))
+
+        def kept(shape, dtype, name):
+            return keep.tile(shape, dtype, name=name, align_bytes=64)
+
+        def load_list(src, n, name):
+            tile = keep.tile([P, n // 16], U16, name=name)
+            nc.sync.dma_start(tile[:], src)
+            return tile
+
+        def load_scale_rows(queue, plane, src):
+            for q in range(4):
+                queue.dma_start(plane[32 * q : 32 * q + 4].bitcast(I32),
+                                src[:, 4 * q : 4 * q + 4, :].rearrange("a r n -> r a n").bitcast(I32))
+
+        tab2_s = kept([P, 1, T3], U8, "tab2_s")
+        wf_s_raw = kept([P, 1, H], U8, "wf_s_raw")
+        tab_s = kept([P, 2, T], U8, "tab_s")
+        wv_s_raw = kept([P, 2, H], U8, "wv_s_raw")
+        nc.vector.memset(tab2_s[:].bitcast(I32), 0)
+        nc.gpsimd.memset(wf_s_raw[:].bitcast(I32), 0)
+        nc.vector.memset(tab_s[:].bitcast(I32), 0)
+        nc.gpsimd.memset(wv_s_raw[:].bitcast(I32), 0)
+
+        l2 = load_list(offs2, S, "l2")
+        tab2_w = kept([P, T3], U32, "tab2_w")
+        nc.sync.dma_start(tab2_w[:].bitcast(I32), tab2_words[0].rearrange("p t i -> p (t i)").bitcast(I32))
+        load_scale_rows(nc.scalar, tab2_s, tab2_scales)
+        load_scale_rows(nc.gpsimd, wf_s_raw, wf_scales)
+        wf_raw = ring.tile([P, H], I32, name="wf_raw", tag="raw", bufs=3, align_bytes=64)
+        nc.sync.dma_start(wf_raw[:], wf_words[0].rearrange("p c i -> p (c i)").bitcast(I32))
+        l4 = load_list(offs4, S, "l4")
+
+        v2_w = kept([P, S], U32, "v2_w")
+        v2_s = kept([P, S], U8, "v2_s")
+        nc.vector.tensor_copy(v2_w[:], tab2_w[:].indirect(l2[:]))
+        wf_w = kept([P, H], I32, "wf_w")
+        wf_s = kept([P, H], U8, "wf_s")
+        nc.vector.tensor_copy(wf_w[:].rearrange("p (b t m) -> p b m t", b=2, t=4),
+                              wf_raw[:].rearrange("p (b m t) -> p b m t", b=2, t=4))
+        nc.vector.tensor_copy(v2_s[:], tab2_s[:, 0, :].indirect(l2[:]))
+        nc.vector.tensor_copy(wf_s[:].rearrange("p (b t m) -> p b t m", b=2, t=4),
+                              wf_s_raw[:, 0, :].rearrange("p (b m t) -> p b t m", b=2, t=4))
+
+        pages = {}
+        floor_rows = {}
+
+        def load_slice(s):
+            b, t = divmod(s, 4)
+            floor_rows[s] = ring.tile([P, S], F32, name="floor", bufs=3)
+            nc.sync.dma_start(floor_rows[s][:], floors.rearrange("(b p t) j -> b t p j", b=2, t=4)[b, t])
+            pages[s] = ring.tile([P, T2], F32, name="page", bufs=5)
+            nc.sync.dma_start(pages[s][:], page0.rearrange("(b p t) j -> b t p j", b=2, t=4)[b, t])
+
+        def load_gate(src, name):
+            tile = kept([P, 4, S], F32, name)
+            for q in range(4):
+                nc.sync.dma_start(tile[32 * q : 32 * (q + 1)], src.rearrange("(m t) j -> m t j", t=4))
+            return tile
+
+        g2 = load_gate(wg2, "g2")
+        load_slice(0)
+        load_slice(1)
+
+        l1 = load_list(offs, S, "l1")
+        load_scale_rows(nc.gpsimd, tab_s, tab_scales)
+        load_scale_rows(nc.gpsimd, wv_s_raw, wv_scales)
+        tab_w = []
+        for a in range(2):
+            tab_w.append(kept([P, T], U32, "tab_w%d" % a))
+            nc.sync.dma_start(tab_w[a][:].bitcast(I32), tab_words[a].rearrange("p t i -> p (t i)").bitcast(I32))
+        wv_raw = ring.tile([P, 2, H // 2], I32, name="wv_raw", tag="raw", bufs=3, align_bytes=64)
+        nc.sync.dma_start(wv_raw[:], wv_words.rearrange("a p c -> p a c").bitcast(I32))
+
+        def load_weight(w, a, b):
+            raw = ring.tile([P, 4, HALF], F32, name="w_raw", tag="raw", bufs=3, align_bytes=64)
+            nc.sync.dma_start(raw[:], w[512 * a : 512 * (a + 1), 512 * b : 512 * (b + 1)].rearrange("(p i) c -> p i c", i=4))
+            return raw
+
+        def quantise_weight(raw, name):
+            grouped = ring.tile([P, 4 * HALF], BF16, name="w_grouped", tag="grouped", bufs=3, align_bytes=64)
+            nc.scalar.copy(grouped[:].rearrange("p (t m i) -> p m t i", t=4, i=4),
+                           raw[:].rearrange("p i (m t) -> p m t i", t=4))
+            codes = kept([P, HALF], U32, name + "_w")
+            scales = kept([P, HALF], U8, name + "_s")
+            nc.vector.quantize_mx(codes[:].bitcast(FP8X4), scales[:], grouped[:])
+            return codes, scales
+
+        wt_q = {}
+        wo_q = {}
+        wt_raw = [load_weight(wt, a, 0) for a in range(2)]
+        l3 = load_list(offs3, S, "l3")
+        l5 = load_list(offs5, NP, "l5")
+        g1 = load_gate(wg1, "g1")
+        shift_col = kept([P, 2, 4], F32, "shift_col")
+        nc.sync.dma_start(shift_col[:], shift.rearrange("(b p t) -> p b t", b=2, t=4))
+        gy_col = kept([P, 2, 4], F32, "gy_col")
+        nc.sync.dma_start(gy_col[:], gy.rearrange("(b p t) -> p b t", b=2, t=4))
+
+        f_ps = {}
+        h2 = {}
+        h1 = {}
+
+        def friction(s):
+            cols = slice(128 * s, 128 * (s + 1))
+            ps = psum.tile([P, S], F32, name="f_ps")
+            nc.tensor.matmul_mx(ps[:], lhsT=wf_w[:, cols].bitcast(FP8X4), lhsT_scale=wf_s[:, cols],
+                                rhs=v2_w[:].bitcast(FP8X4), rhs_scale=v2_s[:], start=True, stop=True)
+            h2[s] = ring.tile([P, S], F32, name="h2")
+            nc.vector.tensor_tensor(h2[s][:], ps[:], floor_rows[s][:], ALU.max)
+
+        def put_friction(s):
+            nc.vector.tensor_tensor(pages[s][:].indirect(l4[:]), h2[s][:], g2[:, s % 4, :], ALU.mult)
+
+        friction(0)
+        put_friction(0)
+        friction(1)
+        put_friction(1)
+
+        v_w, v_s = [], []
+        for a in range(2):
+            v_w.append(kept([P, S], U32, "v_w%d" % a))
+            v_s.append(kept([P, S], U8, "v_s%d" % a))
+            nc.vector.tensor_copy(v_w[a][:], tab_w[a][:].indirect(l1[:]))
+            nc.vector.tensor_copy(v_s[a][:], tab_s[:, a, :].indirect(l1[:]))
+        wv_w = kept([P, 2 * H], U16, "wv_w")
+        wv_s = kept([P, 2 * H], U8, "wv_s")
+        nc.vector.tensor_copy(wv_w[:].rearrange("p (c t m) -> p c m t", c=4, t=4),
+                              wv_raw[:].rearrange("p a c -> p (a c)").bitcast(U16).rearrange("p (c m t) -> p c m t", c=4, t=4))
+        nc.vector.tensor_copy(wv_s[:].rearrange("p (c t m) -> p c t m", c=4, t=4),
+                              wv_s_raw[:].rearrange("p a (b m t) -> p (a b) t m", b=2, t=4))
+        for a in range(2):
+            wt_q[a, 0] = quantise_weight(wt_raw[a], "wt%d0" % a)
+
+        def snow(s):
+            b, t = divmod(s, 4)
+            a_ps = psum.tile([P, S], F32, name="a_ps")
+            s_ps = psum.tile([P, S], F32, name="s_ps")
+            tcols = slice(128 * t, 128 * (t + 1))
+            for a in range(2):
+                codes, scales = wt_q[a, b]
+                nc.tensor.matmul_mx(a_ps[:], lhsT=codes[:, tcols].bitcast(FP8X4), lhsT_scale=scales[:, tcols],
+                                    rhs=v_w[a][:].bitcast(FP8X4), rhs_scale=v_s[a][:], start=(a == 0), stop=(a == 1))
+            for a in range(2):
+                cols = slice(H * a + 128 * s, H * a + 128 * (s + 1))
+                nc.tensor.matmul_mx(s_ps[:], lhsT=wv_w[:, cols].bitcast(FP4X4), lhsT_scale=wv_s[:, cols],
+                                    rhs=v_w[a][:].bitcast(FP8X4), rhs_scale=v_s[a][:], start=(a == 0), stop=(a == 1))
+            th = ring.tile([P, S], F32, name="th", tag="tanh", bufs=3)
+            nc.scalar.activation(th[:], a_ps[:], ACT.Tanh)
+            h1[s] = ring.tile([P, S], F32, name="h1")
+            nc.vector.tensor_tensor(h1[s][:], s_ps[:], th[:], ALU.mult)
+
+        def put_snow(s):
+            nc.vector.tensor_tensor(pages[s][:].indirect(l3[:]), h1[s][:], g1[:, s % 4, :], ALU.mult)
+
+        slots = {(b, h): kept([P, 4, HALF], F32, "slots%d%d" % (b, h)) for b in range(2) for h in range(2)}
+        x_grouped = {}
+        x_q = {}
+
+        def fetch(s):
+            b, t = divmod(s, 4)
+            for h in range(2):
+                if t == 0:
+                    x_grouped[b, h] = ring.tile([P, HALF, 4], BF16, name="x_grouped", bufs=2, align_bytes=64)
+                nc.vector.tensor_copy(slots[b, h][:, t, :], pages[s][:].indirect(l5[:, 32 * h : 32 * (h + 1)]))
+                nc.scalar.activation(x_grouped[b, h][:, :, t], slots[b, h][:, t, :], ACT.Identity,
+                                     bias=shift_col[:, b, t : t + 1])
+
+        def quantise_x(b, h):
+            codes = kept([P, HALF], U32, "x%d%d_w" % (b, h))
+            scales = kept([P, HALF], U8, "x%d%d_s" % (b, h))
+            nc.vector.quantize_mx(codes[:].bitcast(FP8X4), scales[:], x_grouped[b, h][:].rearrange("p j t -> p (j t)"))
+            x_q[b, h] = codes, scales
+
+        later_weights = {1: [(wt, wt_q, 0, 1, "wt01"), (wt, wt_q, 1, 1, "wt11")],
+                         3: [(wo, wo_q, 0, 0, "wo00"), (wo, wo_q, 0, 1, "wo01")],
+                         4: [(wo, wo_q, 1, 0, "wo10"), (wo, wo_q, 1, 1, "wo11")]}
+        snow(0)
+        for s in range(8):
+            if s + 2 < 8:
+                load_slice(s + 2)
+            if s >= 2:
+                put_friction(s)
+            if 2 <= s + 1 < 8:
+                friction(s + 1)
+            put_snow(s)
+            for w, table, a, b, name in later_weights.get(s, []):
+                table[a, b] = quantise_weight(load_weight(w, a, b), name)
+            if s + 1 < 8:
+                snow(s + 1)
+            fetch(s)
+            if s == 3:
+                quantise_x(0, 0)
+                quantise_x(0, 1)
+
+        y_s = [kept([P, 2, HALF], U8, "y_s%d" % h) for h in range(2)]
+
+        def z_pass(ps, g, t, h, b):
+            codes, scales = wo_q[b, g]
+            tcols = slice(128 * t, 128 * (t + 1))
+            nc.tensor.matmul_mx(ps[:], lhsT=codes[:, tcols].bitcast(FP8X4), lhsT_scale=scales[:, tcols],
+                                rhs=x_q[b, h][0][:].bitcast(FP8X4), rhs_scale=x_q[b, h][1][:],
+                                start=(b == 0), stop=(b == 1))
+
+        for h in range(2):
+            quantise_x(1, h)
+        for h in range(2):
+            cols = slice(HALF * h, HALF * (h + 1))
+            for g in range(2):
+                y = slots[g, h]
+                banks = [psum.tile([P, HALF], F32, name="z_ps", bufs=5) for t in range(4)]
+                for t in range(4):
+                    z_pass(banks[t], g, t, h, 0)
+                for t in range(4):
+                    z_pass(banks[t], g, t, h, 1)
+                    tz = ring.tile([P, HALF], F32, name="tz", tag="tanh", bufs=3)
+                    nc.scalar.activation(tz[:], banks[t][:], ACT.Tanh)
+                    nc.vector.scalar_tensor_tensor(y[:, t, :], y[:, t, :], gy_col[:, g, t : t + 1], tz[:], ALU.mult, ALU.add)
+                nc.sync.dma_start(out_0[512 * g : 512 * (g + 1), cols].rearrange("(p t) j -> p t j", t=4), y[:])
+                grouped = ring.tile([P, HALF, 4], BF16, name="y_grouped", tag="grouped", bufs=3, align_bytes=64)
+                nc.vector.tensor_copy(grouped[:, :Y_VEC, :].rearrange("p (c i) t -> p c t i", i=4),
+                                      y[:, :, :Y_VEC].rearrange("p t (c i) -> p c t i", i=4))
+                nc.scalar.copy(grouped[:, Y_VEC:, :].rearrange("p (c i) t -> p c t i", i=4),
+                               y[:, :, Y_VEC:].rearrange("p t (c i) -> p c t i", i=4))
+                codes = kept([P, HALF], U32, "y%d%d_w" % (g, h))
+                nc.vector.quantize_mx(codes[:].bitcast(FP8X4), y_s[h][:, g, :], grouped[:].rearrange("p j t -> p (j t)"))
+                nc.sync.dma_start(out_1[g].rearrange("p m t -> p (m t)")[:, 4 * HALF * h : 4 * HALF * (h + 1)].bitcast(I32),
+                                  codes[:].bitcast(I32))
+            for q in range(4):
+                nc.sync.dma_start(out_2[:, 4 * q : 4 * q + 4, cols].rearrange("g r m -> r g m").bitcast(I32),
+                                  y_s[h][32 * q : 32 * q + 4].bitcast(I32))

@@ -19,6 +19,7 @@ ALU = mybir.AluOpType
 P = 128
 HALF = 512
 Y_VEC = 256
+Y_VEC_LAST = 352
 
 
 def tile_list_glide_slab_page_kernel(
@@ -32,137 +33,135 @@ def tile_list_glide_slab_page_kernel(
         ring = ctx.enter_context(tc.tile_pool(name="ring", bufs=1))
         psum = ctx.enter_context(tc.psum_pool(name="psum", bufs=1))
 
-        def kept(shape, dtype, name):
-            return keep.tile(shape, dtype, name=name, align_bytes=64)
+        def kept(shape, dtype, name, tag=""):
+            return keep.tile(shape, dtype, name=name, tag=tag or name, align_bytes=64)
 
         def load_list(src, n, name):
             tile = keep.tile([P, n // 16], U16, name=name)
             nc.sync.dma_start(tile[:], src)
             return tile
 
-        def load_scale_rows(queue, plane, src):
+        def load_scale_rows(plane, src):
+            passes = src.shape[0]
             for q in range(4):
-                queue.dma_start(plane[32 * q : 32 * q + 4].bitcast(I32),
-                                src[:, 4 * q : 4 * q + 4, :].rearrange("a r n -> r a n").bitcast(I32))
+                nc.sync.dma_start(plane[32 * q : 32 * q + 4, :].rearrange("r (a n) -> r a n", a=passes),
+                                  src[:, 4 * q : 4 * q + 4, :].rearrange("a r n -> r a n").bitcast(I32))
 
-        tab2_s = kept([P, 1, T3], U8, "tab2_s")
-        wf_s_raw = kept([P, 1, H], U8, "wf_s_raw")
-        tab_s = kept([P, 2, T], U8, "tab_s")
-        wv_s_raw = kept([P, 2, H], U8, "wv_s_raw")
-        nc.vector.memset(tab2_s[:].bitcast(I32), 0)
-        nc.gpsimd.memset(wf_s_raw[:].bitcast(I32), 0)
-        nc.vector.memset(tab_s[:].bitcast(I32), 0)
-        nc.gpsimd.memset(wv_s_raw[:].bitcast(I32), 0)
-
-        l2 = load_list(offs2, S, "l2")
-        tab2_w = kept([P, T3], U32, "tab2_w")
-        nc.sync.dma_start(tab2_w[:].bitcast(I32), tab2_words[0].rearrange("p t i -> p (t i)").bitcast(I32))
-        load_scale_rows(nc.scalar, tab2_s, tab2_scales)
-        load_scale_rows(nc.gpsimd, wf_s_raw, wf_scales)
-        wf_raw = ring.tile([P, H], I32, name="wf_raw", tag="raw", bufs=3, align_bytes=64)
-        nc.sync.dma_start(wf_raw[:], wf_words[0].rearrange("p c i -> p (c i)").bitcast(I32))
-        l4 = load_list(offs4, S, "l4")
-
-        v2_w = kept([P, S], U32, "v2_w")
-        v2_s = kept([P, S], U8, "v2_s")
-        nc.vector.tensor_copy(v2_w[:], tab2_w[:].indirect(l2[:]))
-        wf_w = kept([P, H], I32, "wf_w")
-        wf_s = kept([P, H], U8, "wf_s")
-        nc.vector.tensor_copy(wf_w[:].rearrange("p (b t m) -> p b m t", b=2, t=4),
-                              wf_raw[:].rearrange("p (b m t) -> p b m t", b=2, t=4))
-        nc.vector.tensor_copy(v2_s[:], tab2_s[:, 0, :].indirect(l2[:]))
-        nc.vector.tensor_copy(wf_s[:].rearrange("p (b t m) -> p b t m", b=2, t=4),
-                              wf_s_raw[:, 0, :].rearrange("p (b m t) -> p b t m", b=2, t=4))
+        tab2_s = kept([P, T3 // 4], I32, "tab2_s")
+        wf_s_raw = kept([P, H // 4], I32, "wf_s_raw")
+        tab_s = kept([P, 2 * T // 4], I32, "tab_s")
+        wv_s_raw = kept([P, 2 * H // 4], I32, "wv_s_raw")
+        for plane in [wf_s_raw, tab2_s, tab_s, wv_s_raw]:
+            nc.vector.memset(plane[:], 0)
 
         pages = {}
-        floor_rows = {}
+        h2 = {}
+        h1 = {}
 
-        def load_slice(s):
+        def load_floor(s):
             b, t = divmod(s, 4)
-            floor_rows[s] = ring.tile([P, S], F32, name="floor", bufs=3)
-            nc.sync.dma_start(floor_rows[s][:], floors.rearrange("(b p t) j -> b t p j", b=2, t=4)[b, t])
+            h2[s] = kept([P, S], F32, "floor%d" % s, tag="row%d" % s)
+            nc.sync.dma_start(h2[s][:], floors.rearrange("(b p t) j -> b t p j", b=2, t=4)[b, t])
+
+        def load_page(s):
+            b, t = divmod(s, 4)
             pages[s] = ring.tile([P, T2], F32, name="page", bufs=5)
             nc.sync.dma_start(pages[s][:], page0.rearrange("(b p t) j -> b t p j", b=2, t=4)[b, t])
 
-        def load_gate(src, name):
-            tile = kept([P, 4, S], F32, name)
+        def load_gate(src, t0, t1, name):
+            tile = kept([P, t1 - t0, S], F32, name)
             for q in range(4):
-                nc.sync.dma_start(tile[32 * q : 32 * (q + 1)], src.rearrange("(m t) j -> m t j", t=4))
-            return tile
-
-        g2 = load_gate(wg2, "g2")
-        load_slice(0)
-        load_slice(1)
-
-        l1 = load_list(offs, S, "l1")
-        load_scale_rows(nc.gpsimd, tab_s, tab_scales)
-        load_scale_rows(nc.gpsimd, wv_s_raw, wv_scales)
-        tab_w = []
-        for a in range(2):
-            tab_w.append(kept([P, T], U32, "tab_w%d" % a))
-            nc.sync.dma_start(tab_w[a][:].bitcast(I32), tab_words[a].rearrange("p t i -> p (t i)").bitcast(I32))
-        wv_raw = ring.tile([P, 2, H // 2], I32, name="wv_raw", tag="raw", bufs=3, align_bytes=64)
-        nc.sync.dma_start(wv_raw[:], wv_words.rearrange("a p c -> p a c").bitcast(I32))
+                nc.sync.dma_start(tile[32 * q : 32 * (q + 1)], src.rearrange("(m t) j -> m t j", t=4)[:, t0:t1, :])
+            return [tile[:, t, :] for t in range(t1 - t0)]
 
         def load_weight(w, a, b):
             raw = ring.tile([P, 4, HALF], F32, name="w_raw", tag="raw", bufs=3, align_bytes=64)
             nc.sync.dma_start(raw[:], w[512 * a : 512 * (a + 1), 512 * b : 512 * (b + 1)].rearrange("(p i) c -> p i c", i=4))
             return raw
 
-        def quantise_weight(raw, name):
+        def load_table(a):
+            tile = kept([P, T], U32, "tab_w%d" % a)
+            nc.sync.dma_start(tile[:].bitcast(I32), tab_words[a].rearrange("p t i -> p (t i)").bitcast(I32))
+            return tile
+
+        def round_weight(raw):
             grouped = ring.tile([P, 4 * HALF], BF16, name="w_grouped", tag="grouped", bufs=3, align_bytes=64)
-            nc.scalar.copy(grouped[:].rearrange("p (t m i) -> p m t i", t=4, i=4),
-                           raw[:].rearrange("p i (m t) -> p m t i", t=4))
-            codes = kept([P, HALF], U32, name + "_w")
+            nc.scalar.copy(grouped[:].rearrange("p (t m i) -> p m i t", t=4, i=4),
+                           raw[:].rearrange("p i (m t) -> p m i t", t=4))
+            return grouped[:]
+
+        def quantise(grouped, name, codes=None):
+            if codes is None:
+                codes = kept([P, HALF], U32, name + "_w")[:]
             scales = kept([P, HALF], U8, name + "_s")
-            nc.vector.quantize_mx(codes[:].bitcast(FP8X4), scales[:], grouped[:])
+            nc.vector.quantize_mx(codes.bitcast(FP8X4), scales[:], grouped)
             return codes, scales
 
-        wt_q = {}
-        wo_q = {}
-        wt_raw = [load_weight(wt, a, 0) for a in range(2)]
-        l3 = load_list(offs3, S, "l3")
-        l5 = load_list(offs5, NP, "l5")
-        g1 = load_gate(wg1, "g1")
-        shift_col = kept([P, 2, 4], F32, "shift_col")
-        nc.sync.dma_start(shift_col[:], shift.rearrange("(b p t) -> p b t", b=2, t=4))
-        gy_col = kept([P, 2, 4], F32, "gy_col")
-        nc.sync.dma_start(gy_col[:], gy.rearrange("(b p t) -> p b t", b=2, t=4))
-
-        f_ps = {}
-        h2 = {}
-        h1 = {}
+        v2_w = kept([P, S], U32, "v2_w")
+        v2_s = kept([P, S], U8, "v2_s")
+        wf_w = kept([P, H], I32, "wf_w")
+        wf_s = kept([P, H], U8, "wf_s")
+        wv_w = kept([P, 2 * H], U16, "wv_w")
+        wv_s = kept([P, 2 * H], U8, "wv_s")
 
         def friction(s):
             cols = slice(128 * s, 128 * (s + 1))
             ps = psum.tile([P, S], F32, name="f_ps")
             nc.tensor.matmul_mx(ps[:], lhsT=wf_w[:, cols].bitcast(FP8X4), lhsT_scale=wf_s[:, cols],
                                 rhs=v2_w[:].bitcast(FP8X4), rhs_scale=v2_s[:], start=True, stop=True)
-            h2[s] = ring.tile([P, S], F32, name="h2")
-            nc.vector.tensor_tensor(h2[s][:], ps[:], floor_rows[s][:], ALU.max)
+            nc.vector.tensor_tensor(h2[s][:], ps[:], h2[s][:], ALU.max)
 
         def put_friction(s):
-            nc.vector.tensor_tensor(pages[s][:].indirect(l4[:]), h2[s][:], g2[:, s % 4, :], ALU.mult)
+            nc.vector.tensor_tensor(pages[s][:].indirect(l4[:]), h2[s][:], g2[s % 4], ALU.mult)
 
+        wt_q = {}
+        wo_q = {}
+        v_w = [kept([P, S], U32, "v_w%d" % a) for a in range(2)]
+        v_s = [kept([P, S], U8, "v_s%d" % a) for a in range(2)]
+
+        l2 = load_list(offs2, S, "l2")
+        l4 = load_list(offs4, S, "l4")
+        load_scale_rows(wf_s_raw, wf_scales)
+        nc.vector.tensor_copy(wf_s[:].rearrange("p (b t m) -> p b t m", b=2, t=4),
+                              wf_s_raw[:].bitcast(U8).rearrange("p (b m t) -> p b t m", b=2, t=4))
+        tab2_w = kept([P, T3], U32, "tab2_w")
+        nc.sync.dma_start(tab2_w[:].bitcast(I32), tab2_words[0].rearrange("p t i -> p (t i)").bitcast(I32))
+        nc.vector.tensor_copy(v2_w[:], tab2_w[:].indirect(l2[:]))
+        wf_raw = ring.tile([P, H], I32, name="wf_raw", tag="raw", bufs=3, align_bytes=64)
+        nc.sync.dma_start(wf_raw[:], wf_words[0].rearrange("p c i -> p (c i)").bitcast(I32))
+        nc.vector.tensor_copy(wf_w[:].rearrange("p (b t m) -> p b m t", b=2, t=4),
+                              wf_raw[:].rearrange("p (b m t) -> p b m t", b=2, t=4))
+        load_scale_rows(tab2_s, tab2_scales)
+        nc.vector.tensor_copy(v2_s[:], tab2_s[:].bitcast(U8).indirect(l2[:]))
+        load_floor(0)
         friction(0)
+        load_page(0)
+        g2 = load_gate(wg2, 0, 2, "g2_first")
         put_friction(0)
-        friction(1)
-        put_friction(1)
-
-        v_w, v_s = [], []
-        for a in range(2):
-            v_w.append(kept([P, S], U32, "v_w%d" % a))
-            v_s.append(kept([P, S], U8, "v_s%d" % a))
-            nc.vector.tensor_copy(v_w[a][:], tab_w[a][:].indirect(l1[:]))
-            nc.vector.tensor_copy(v_s[a][:], tab_s[:, a, :].indirect(l1[:]))
-        wv_w = kept([P, 2 * H], U16, "wv_w")
-        wv_s = kept([P, 2 * H], U8, "wv_s")
+        l1 = load_list(offs, S, "l1")
+        wt_q[0, 0] = quantise(round_weight(load_weight(wt, 0, 0)), "wt00")
+        wv_raw = ring.tile([P, 2, H // 2], I32, name="wv_raw", tag="raw", bufs=3, align_bytes=64)
+        nc.sync.dma_start(wv_raw[:], wv_words.rearrange("a p c -> p a c").bitcast(I32))
         nc.vector.tensor_copy(wv_w[:].rearrange("p (c t m) -> p c m t", c=4, t=4),
                               wv_raw[:].rearrange("p a c -> p (a c)").bitcast(U16).rearrange("p (c m t) -> p c m t", c=4, t=4))
+        load_scale_rows(wv_s_raw, wv_scales)
         nc.vector.tensor_copy(wv_s[:].rearrange("p (c t m) -> p c t m", c=4, t=4),
-                              wv_s_raw[:].rearrange("p a (b m t) -> p (a b) t m", b=2, t=4))
+                              wv_s_raw[:].bitcast(U8).rearrange("p (c m t) -> p c t m", c=4, t=4))
+        nc.vector.tensor_copy(v_w[0][:], load_table(0)[:].indirect(l1[:]))
+        load_scale_rows(tab_s, tab_scales)
         for a in range(2):
-            wt_q[a, 0] = quantise_weight(wt_raw[a], "wt%d0" % a)
+            nc.vector.tensor_copy(v_s[a][:], tab_s[:].bitcast(U8)[:, T * a : T * (a + 1)].indirect(l1[:]))
+        wt_q[1, 0] = quantise(round_weight(load_weight(wt, 1, 0)), "wt10")
+        nc.vector.tensor_copy(v_w[1][:], load_table(1)[:].indirect(l1[:]))
+        l3 = load_list(offs3, S, "l3")
+        g1 = load_gate(wg1, 0, 2, "g1_first")
+        load_floor(1)
+        friction(1)
+        load_page(1)
+        put_friction(1)
+        l5 = load_list(offs5, NP, "l5")
+        shift_col = kept([P, 2, 4], F32, "shift_col")
+        nc.sync.dma_start(shift_col[:], shift.rearrange("(b p t) -> p b t", b=2, t=4))
 
         def snow(s):
             b, t = divmod(s, 4)
@@ -177,15 +176,15 @@ def tile_list_glide_slab_page_kernel(
                 cols = slice(H * a + 128 * s, H * a + 128 * (s + 1))
                 nc.tensor.matmul_mx(s_ps[:], lhsT=wv_w[:, cols].bitcast(FP4X4), lhsT_scale=wv_s[:, cols],
                                     rhs=v_w[a][:].bitcast(FP8X4), rhs_scale=v_s[a][:], start=(a == 0), stop=(a == 1))
-            th = ring.tile([P, S], F32, name="th", tag="tanh", bufs=3)
+            th = kept([P, S], F32, "th%d" % s)
             nc.scalar.activation(th[:], a_ps[:], ACT.Tanh)
-            h1[s] = ring.tile([P, S], F32, name="h1")
+            h1[s] = kept([P, S], F32, "h1_%d" % s, tag="row%d" % (s - 1 if s > 0 else 1))
             nc.vector.tensor_tensor(h1[s][:], s_ps[:], th[:], ALU.mult)
 
         def put_snow(s):
-            nc.vector.tensor_tensor(pages[s][:].indirect(l3[:]), h1[s][:], g1[:, s % 4, :], ALU.mult)
+            nc.vector.tensor_tensor(pages[s][:].indirect(l3[:]), h1[s][:], g1[s % 4], ALU.mult)
 
-        slots = {(b, h): kept([P, 4, HALF], F32, "slots%d%d" % (b, h)) for b in range(2) for h in range(2)}
+        slots = {}
         x_grouped = {}
         x_q = {}
 
@@ -193,37 +192,62 @@ def tile_list_glide_slab_page_kernel(
             b, t = divmod(s, 4)
             for h in range(2):
                 if t == 0:
-                    x_grouped[b, h] = ring.tile([P, HALF, 4], BF16, name="x_grouped", bufs=2, align_bytes=64)
+                    slots[b, h] = kept([P, 4, HALF], F32, "slots%d%d" % (b, h), tag="tab_w%d" % h if b == 1 else "")
+                    x_grouped[b, h] = kept([P, HALF, 4], BF16, "x_grouped%d%d" % (b, h))
                 nc.vector.tensor_copy(slots[b, h][:, t, :], pages[s][:].indirect(l5[:, 32 * h : 32 * (h + 1)]))
                 nc.scalar.activation(x_grouped[b, h][:, :, t], slots[b, h][:, t, :], ACT.Identity,
                                      bias=shift_col[:, b, t : t + 1])
 
-        def quantise_x(b, h):
-            codes = kept([P, HALF], U32, "x%d%d_w" % (b, h))
-            scales = kept([P, HALF], U8, "x%d%d_s" % (b, h))
-            nc.vector.quantize_mx(codes[:].bitcast(FP8X4), scales[:], x_grouped[b, h][:].rearrange("p j t -> p (j t)"))
-            x_q[b, h] = codes, scales
+        def x_rows(b, h):
+            return x_grouped[b, h][:].rearrange("p j t -> p (j t)")
 
-        later_weights = {1: [(wt, wt_q, 0, 1, "wt01"), (wt, wt_q, 1, 1, "wt11")],
-                         3: [(wo, wo_q, 0, 0, "wo00"), (wo, wo_q, 0, 1, "wo01")],
-                         4: [(wo, wo_q, 1, 0, "wo10"), (wo, wo_q, 1, 1, "wo11")]}
+        def after_tanh(s, name):
+            return kept([P, HALF], U32, name, tag="th%d" % s)[:]
+
         snow(0)
-        for s in range(8):
-            if s + 2 < 8:
-                load_slice(s + 2)
-            if s >= 2:
-                put_friction(s)
-            if 2 <= s + 1 < 8:
+        put_snow(0)
+        snow(1)
+        fetch(0)
+        rows = round_weight(load_weight(wt, 0, 1))
+        put_snow(1)
+        fetch(1)
+        wt_q[0, 1] = quantise(rows, "wt01", kept([P, HALF], U32, "wt01_w", tag="row0")[:])
+        load_floor(2)
+        g2 = g2 + load_gate(wg2, 2, 4, "g2_rest")
+        friction(2)
+        g1 = g1 + load_gate(wg1, 2, 4, "g1_rest")
+        gy_col = kept([P, 2, 4], F32, "gy_col")
+        nc.sync.dma_start(gy_col[:], gy.rearrange("(b p t) -> p b t", b=2, t=4))
+        snow(2)
+        late_rows = []
+        for s in range(2, 8):
+            if s < 7:
+                a, b = divmod(s - 3, 2)
+                rows = round_weight(load_weight(wt, 1, 1) if s == 2 else load_weight(wo, b, a))
+            load_page(s)
+            put_friction(s)
+            if s < 7:
+                load_floor(s + 1)
                 friction(s + 1)
             put_snow(s)
-            for w, table, a, b, name in later_weights.get(s, []):
-                table[a, b] = quantise_weight(load_weight(w, a, b), name)
-            if s + 1 < 8:
+            if s < 7:
                 snow(s + 1)
             fetch(s)
-            if s == 3:
-                quantise_x(0, 0)
-                quantise_x(0, 1)
+            if s == 2:
+                wt_q[1, 1] = quantise(rows, "wt11", after_tanh(3, "wt11_w"))
+            elif s in (3, 4):
+                wo_q[s - 3, 0] = quantise(rows, "wo%d0" % (s - 3), after_tanh(s + 1, "wo%d0_w" % (s - 3)))
+            elif s in (5, 6):
+                late_rows.append(rows)
+            if s == 5:
+                x_q[0, 0] = quantise(x_rows(0, 0), "x00", after_tanh(6, "x00_w"))
+
+        late_codes = kept([P, 3, HALF], U32, "late_codes", tag="g1_rest")
+        x_q[1, 0] = quantise(x_rows(1, 0), "x10")
+        for a in range(2):
+            wo_q[a, 1] = quantise(late_rows[a], "wo%d1" % a, late_codes[:, a, :])
+        x_q[0, 1] = quantise(x_rows(0, 1), "x01", late_codes[:, 2, :])
+        x_q[1, 1] = quantise(x_rows(1, 1), "x11")
 
         y_s = [kept([P, 2, HALF], U8, "y_s%d" % h) for h in range(2)]
 
@@ -231,29 +255,33 @@ def tile_list_glide_slab_page_kernel(
             codes, scales = wo_q[b, g]
             tcols = slice(128 * t, 128 * (t + 1))
             nc.tensor.matmul_mx(ps[:], lhsT=codes[:, tcols].bitcast(FP8X4), lhsT_scale=scales[:, tcols],
-                                rhs=x_q[b, h][0][:].bitcast(FP8X4), rhs_scale=x_q[b, h][1][:],
+                                rhs=x_q[b, h][0].bitcast(FP8X4), rhs_scale=x_q[b, h][1][:],
                                 start=(b == 0), stop=(b == 1))
 
         for h in range(2):
-            quantise_x(1, h)
-        for h in range(2):
             cols = slice(HALF * h, HALF * (h + 1))
             for g in range(2):
+                last = h == 1 and g == 1
                 y = slots[g, h]
+                y_rows = out_0[512 * g : 512 * (g + 1), cols].rearrange("(p t) j -> p t j", t=4)
                 banks = [psum.tile([P, HALF], F32, name="z_ps", bufs=5) for t in range(4)]
                 for t in range(4):
                     z_pass(banks[t], g, t, h, 0)
                 for t in range(4):
                     z_pass(banks[t], g, t, h, 1)
-                    tz = ring.tile([P, HALF], F32, name="tz", tag="tanh", bufs=3)
+                    tz = ring.tile([P, HALF], F32, name="tz", bufs=3)
                     nc.scalar.activation(tz[:], banks[t][:], ACT.Tanh)
                     nc.vector.scalar_tensor_tensor(y[:, t, :], y[:, t, :], gy_col[:, g, t : t + 1], tz[:], ALU.mult, ALU.add)
-                nc.sync.dma_start(out_0[512 * g : 512 * (g + 1), cols].rearrange("(p t) j -> p t j", t=4), y[:])
+                    if last:
+                        nc.sync.dma_start(y_rows[:, t, :], y[:, t, :])
+                if not last:
+                    nc.sync.dma_start(y_rows, y[:])
+                split = Y_VEC_LAST if last else Y_VEC
                 grouped = ring.tile([P, HALF, 4], BF16, name="y_grouped", tag="grouped", bufs=3, align_bytes=64)
-                nc.vector.tensor_copy(grouped[:, :Y_VEC, :].rearrange("p (c i) t -> p c t i", i=4),
-                                      y[:, :, :Y_VEC].rearrange("p t (c i) -> p c t i", i=4))
-                nc.scalar.copy(grouped[:, Y_VEC:, :].rearrange("p (c i) t -> p c t i", i=4),
-                               y[:, :, Y_VEC:].rearrange("p t (c i) -> p c t i", i=4))
+                nc.vector.tensor_copy(grouped[:, :split, :].rearrange("p (c i) t -> p c t i", i=4),
+                                      y[:, :, :split].rearrange("p t (c i) -> p c t i", i=4))
+                nc.scalar.copy(grouped[:, split:, :].rearrange("p (c i) t -> p c t i", i=4),
+                               y[:, :, split:].rearrange("p t (c i) -> p c t i", i=4))
                 codes = kept([P, HALF], U32, "y%d%d_w" % (g, h))
                 nc.vector.quantize_mx(codes[:].bitcast(FP8X4), y_s[h][:, g, :], grouped[:].rearrange("p j t -> p (j t)"))
                 nc.sync.dma_start(out_1[g].rearrange("p m t -> p (m t)")[:, 4 * HALF * h : 4 * HALF * (h + 1)].bitcast(I32),

@@ -84,11 +84,24 @@ def tile_list_glide_slab_page_kernel(
             nc.sync.dma_start(tile[:].bitcast(I32), tab_words[a].rearrange("p t i -> p (t i)").bitcast(I32))
             return tile
 
+        def round_columns(grouped, raw, t0, t1):
+            nc.scalar.copy(grouped[:, HALF * t0 : HALF * t1].rearrange("p (t m i) -> p m t i", t=t1 - t0, i=4),
+                           raw[:].rearrange("p i (m t) -> p m t i", t=4)[:, :, t0:t1, :])
+
         def round_weight(raw):
             grouped = ring.tile([P, 4 * HALF], BF16, name="w_grouped", tag="grouped", bufs=3, align_bytes=64)
-            nc.scalar.copy(grouped[:].rearrange("p (t m i) -> p m i t", t=4, i=4),
-                           raw[:].rearrange("p i (m t) -> p m i t", t=4))
+            round_columns(grouped, raw, 0, 4)
             return grouped[:]
+
+        def quantise_by_slices(raw, name):
+            grouped = ring.tile([P, 4 * HALF], BF16, name="w_grouped", tag="grouped", bufs=3, align_bytes=64)
+            codes = kept([P, HALF], U32, name + "_w")
+            scales = kept([P, HALF], U8, name + "_s")
+            for t0, t1 in ((0, 1), (1, 2), (2, 4)):
+                round_columns(grouped, raw, t0, t1)
+                nc.vector.quantize_mx(codes[:, P * t0 : P * t1].bitcast(FP8X4), scales[:, P * t0 : P * t1],
+                                      grouped[:, HALF * t0 : HALF * t1])
+            return codes[:], scales
 
         def quantise(grouped, name, codes=None):
             if codes is None:
@@ -136,29 +149,27 @@ def tile_list_glide_slab_page_kernel(
         load_floor(0)
         friction(0)
         load_page(0)
-        g2 = load_gate(wg2, 0, 2, "g2_first")
+        g2 = load_gate(wg2, 0, 1, "g2_first")
         put_friction(0)
         l1 = load_list(offs, S, "l1")
-        wt_q[0, 0] = quantise(round_weight(load_weight(wt, 0, 0)), "wt00")
         wv_raw = ring.tile([P, 2, H // 2], I32, name="wv_raw", tag="raw", bufs=3, align_bytes=64)
         nc.sync.dma_start(wv_raw[:], wv_words.rearrange("a p c -> p a c").bitcast(I32))
-        nc.vector.tensor_copy(wv_w[:].rearrange("p (c t m) -> p c m t", c=4, t=4),
-                              wv_raw[:].rearrange("p a c -> p (a c)").bitcast(U16).rearrange("p (c m t) -> p c m t", c=4, t=4))
+        nc.vector.tensor_copy(wv_w[:].rearrange("p (c t m) -> p c t m", c=4, t=4),
+                              wv_raw[:].rearrange("p a c -> p (a c)").bitcast(U16).rearrange("p (c m t) -> p c t m", c=4, t=4))
         load_scale_rows(wv_s_raw, wv_scales)
         nc.vector.tensor_copy(wv_s[:].rearrange("p (c t m) -> p c t m", c=4, t=4),
                               wv_s_raw[:].bitcast(U8).rearrange("p (c m t) -> p c t m", c=4, t=4))
+        wt_q[0, 0] = quantise(round_weight(load_weight(wt, 0, 0)), "wt00")
         nc.vector.tensor_copy(v_w[0][:], load_table(0)[:].indirect(l1[:]))
         load_scale_rows(tab_s, tab_scales)
         for a in range(2):
             nc.vector.tensor_copy(v_s[a][:], tab_s[:].bitcast(U8)[:, T * a : T * (a + 1)].indirect(l1[:]))
-        wt_q[1, 0] = quantise(round_weight(load_weight(wt, 1, 0)), "wt10")
         nc.vector.tensor_copy(v_w[1][:], load_table(1)[:].indirect(l1[:]))
+        wt_q[1, 0] = quantise_by_slices(load_weight(wt, 1, 0), "wt10")
         l3 = load_list(offs3, S, "l3")
-        g1 = load_gate(wg1, 0, 2, "g1_first")
+        g1 = load_gate(wg1, 0, 1, "g1_first")
         load_floor(1)
         friction(1)
-        load_page(1)
-        put_friction(1)
         l5 = load_list(offs5, NP, "l5")
         shift_col = kept([P, 2, 4], F32, "shift_col")
         nc.sync.dma_start(shift_col[:], shift.rearrange("(b p t) -> p b t", b=2, t=4))
@@ -178,7 +189,7 @@ def tile_list_glide_slab_page_kernel(
                                     rhs=v_w[a][:].bitcast(FP8X4), rhs_scale=v_s[a][:], start=(a == 0), stop=(a == 1))
             th = kept([P, S], F32, "th%d" % s)
             nc.scalar.activation(th[:], a_ps[:], ACT.Tanh)
-            h1[s] = kept([P, S], F32, "h1_%d" % s, tag="row%d" % (s - 1 if s > 0 else 1))
+            h1[s] = kept([P, S], F32, "h1_%d" % s, tag="row%d" % (s - 1) if s > 0 else "")
             nc.vector.tensor_tensor(h1[s][:], s_ps[:], th[:], ALU.mult)
 
         def put_snow(s):
@@ -208,20 +219,10 @@ def tile_list_glide_slab_page_kernel(
         put_snow(0)
         snow(1)
         fetch(0)
-        rows = round_weight(load_weight(wt, 0, 1))
-        put_snow(1)
-        fetch(1)
-        wt_q[0, 1] = quantise(rows, "wt01", kept([P, HALF], U32, "wt01_w", tag="row0")[:])
-        load_floor(2)
-        g2 = g2 + load_gate(wg2, 2, 4, "g2_rest")
-        friction(2)
-        g1 = g1 + load_gate(wg1, 2, 4, "g1_rest")
-        gy_col = kept([P, 2, 4], F32, "gy_col")
-        nc.sync.dma_start(gy_col[:], gy.rearrange("(b p t) -> p b t", b=2, t=4))
-        snow(2)
+        g2 = g2 + load_gate(wg2, 1, 4, "g2_rest")
         late_rows = []
-        for s in range(2, 8):
-            if s < 7:
+        for s in range(1, 8):
+            if 1 < s < 7:
                 a, b = divmod(s - 3, 2)
                 rows = round_weight(load_weight(wt, 1, 1) if s == 2 else load_weight(wo, b, a))
             load_page(s)
@@ -229,11 +230,18 @@ def tile_list_glide_slab_page_kernel(
             if s < 7:
                 load_floor(s + 1)
                 friction(s + 1)
+            if s == 1:
+                g1 = g1 + load_gate(wg1, 1, 4, "g1_rest")
+                gy_col = kept([P, 2, 4], F32, "gy_col")
+                nc.sync.dma_start(gy_col[:], gy.rearrange("(b p t) -> p b t", b=2, t=4))
             put_snow(s)
             if s < 7:
                 snow(s + 1)
             fetch(s)
-            if s == 2:
+            if s == 1:
+                wt01_rows = round_weight(load_weight(wt, 0, 1))
+            elif s == 2:
+                wt_q[0, 1] = quantise(wt01_rows, "wt01", kept([P, HALF], U32, "wt01_w", tag="row1")[:])
                 wt_q[1, 1] = quantise(rows, "wt11", after_tanh(3, "wt11_w"))
             elif s in (3, 4):
                 wo_q[s - 3, 0] = quantise(rows, "wo%d0" % (s - 3), after_tanh(s + 1, "wo%d0_w" % (s - 3)))

@@ -19,7 +19,7 @@ ALU = mybir.AluOpType
 P = 128
 HALF = 512
 Y_VEC = 256
-Y_VEC_LAST = 352
+Y_VEC_LAST = 176
 
 
 def tile_list_glide_slab_page_kernel(
@@ -187,10 +187,15 @@ def tile_list_glide_slab_page_kernel(
                 cols = slice(H * a + 128 * s, H * a + 128 * (s + 1))
                 nc.tensor.matmul_mx(s_ps[:], lhsT=wv_w[:, cols].bitcast(FP4X4), lhsT_scale=wv_s[:, cols],
                                     rhs=v_w[a][:].bitcast(FP8X4), rhs_scale=v_s[a][:], start=(a == 0), stop=(a == 1))
-            th = kept([P, S], F32, "th%d" % s)
+            th = ring.tile([P, S], F32, name="th", bufs=3)
             nc.scalar.activation(th[:], a_ps[:], ACT.Tanh)
-            h1[s] = kept([P, S], F32, "h1_%d" % s, tag="row%d" % (s - 1) if s > 0 else "")
-            nc.vector.tensor_tensor(h1[s][:], s_ps[:], th[:], ALU.mult)
+            h1[s] = ring.tile([P, S], F32, name="h1")
+            if s == 0:
+                nc.vector.tensor_tensor(h1[s][:], s_ps[:], th[:], ALU.mult)
+            else:
+                sn = ring.tile([P, S], F32, name="sn", bufs=2)
+                nc.scalar.copy(sn[:], s_ps[:])
+                nc.gpsimd.tensor_tensor(h1[s][:], sn[:], th[:], ALU.mult)
 
         def put_snow(s):
             nc.vector.tensor_tensor(pages[s][:].indirect(l3[:]), h1[s][:], g1[s % 4], ALU.mult)
@@ -212,8 +217,8 @@ def tile_list_glide_slab_page_kernel(
         def x_rows(b, h):
             return x_grouped[b, h][:].rearrange("p j t -> p (j t)")
 
-        def after_tanh(s, name):
-            return kept([P, HALF], U32, name, tag="th%d" % s)[:]
+        def after_floor(s, count, name):
+            return kept([P, count, HALF], U32, name, tag="row%d" % s)
 
         snow(0)
         put_snow(0)
@@ -237,18 +242,20 @@ def tile_list_glide_slab_page_kernel(
             put_snow(s)
             if s < 7:
                 snow(s + 1)
+            if s == 2:
+                codes = after_floor(s, 2, "wt_1_w")
+                wt_q[0, 1] = quantise(wt01_rows, "wt01", codes[:, 0, :])
+            elif s in (3, 4):
+                wo_q[s - 3, 0] = quantise(rows, "wo%d0" % (s - 3), after_floor(s, 1, "wo%d0_w" % (s - 3))[:, 0, :])
+            elif s in (5, 6):
+                late_rows.append(rows)
+            if s == 5:
+                x_q[0, 0] = quantise(x_rows(0, 0), "x00", after_floor(s, 1, "x00_w")[:, 0, :])
             fetch(s)
             if s == 1:
                 wt01_rows = round_weight(load_weight(wt, 0, 1))
             elif s == 2:
-                wt_q[0, 1] = quantise(wt01_rows, "wt01", kept([P, HALF], U32, "wt01_w", tag="row1")[:])
-                wt_q[1, 1] = quantise(rows, "wt11", after_tanh(3, "wt11_w"))
-            elif s in (3, 4):
-                wo_q[s - 3, 0] = quantise(rows, "wo%d0" % (s - 3), after_tanh(s + 1, "wo%d0_w" % (s - 3)))
-            elif s in (5, 6):
-                late_rows.append(rows)
-            if s == 5:
-                x_q[0, 0] = quantise(x_rows(0, 0), "x00", after_tanh(6, "x00_w"))
+                wt_q[1, 1] = quantise(rows, "wt11", codes[:, 1, :])
 
         late_codes = kept([P, 3, HALF], U32, "late_codes", tag="g1_rest")
         x_q[1, 0] = quantise(x_rows(1, 0), "x10")
@@ -266,6 +273,13 @@ def tile_list_glide_slab_page_kernel(
                                 rhs=x_q[b, h][0].bitcast(FP8X4), rhs_scale=x_q[b, h][1][:],
                                 start=(b == 0), stop=(b == 1))
 
+        planes = []
+
+        def store_planes():
+            for dst, src in planes:
+                nc.sync.dma_start(dst.bitcast(I32), src.bitcast(I32))
+            planes.clear()
+
         for h in range(2):
             cols = slice(HALF * h, HALF * (h + 1))
             for g in range(2):
@@ -280,20 +294,22 @@ def tile_list_glide_slab_page_kernel(
                     tz = ring.tile([P, HALF], F32, name="tz", bufs=3)
                     nc.scalar.activation(tz[:], banks[t][:], ACT.Tanh)
                     nc.vector.scalar_tensor_tensor(y[:, t, :], y[:, t, :], gy_col[:, g, t : t + 1], tz[:], ALU.mult, ALU.add)
-                    if last:
-                        nc.sync.dma_start(y_rows[:, t, :], y[:, t, :])
-                if not last:
-                    nc.sync.dma_start(y_rows, y[:])
-                split = Y_VEC_LAST if last else Y_VEC
+                    nc.sync.dma_start(y_rows[:, t, :], y[:, t, :])
+                    if t == 1:
+                        store_planes()
                 grouped = ring.tile([P, HALF, 4], BF16, name="y_grouped", tag="grouped", bufs=3, align_bytes=64)
-                nc.vector.tensor_copy(grouped[:, :split, :].rearrange("p (c i) t -> p c t i", i=4),
-                                      y[:, :, :split].rearrange("p t (c i) -> p c t i", i=4))
-                nc.scalar.copy(grouped[:, split:, :].rearrange("p (c i) t -> p c t i", i=4),
-                               y[:, :, split:].rearrange("p t (c i) -> p c t i", i=4))
                 codes = kept([P, HALF], U32, "y%d%d_w" % (g, h))
-                nc.vector.quantize_mx(codes[:].bitcast(FP8X4), y_s[h][:, g, :], grouped[:].rearrange("p j t -> p (j t)"))
-                nc.sync.dma_start(out_1[g].rearrange("p m t -> p (m t)")[:, 4 * HALF * h : 4 * HALF * (h + 1)].bitcast(I32),
-                                  codes[:].bitcast(I32))
+                pieces = [(0, Y_VEC_LAST, 256), (256, 256 + Y_VEC_LAST, HALF)] if last else [(0, Y_VEC, HALF)]
+                for c0, c1, c2 in pieces:
+                    nc.vector.tensor_copy(grouped[:, c0:c1, :].rearrange("p (c i) t -> p c t i", i=4),
+                                          y[:, :, c0:c1].rearrange("p t (c i) -> p c t i", i=4))
+                    nc.scalar.copy(grouped[:, c1:c2, :].rearrange("p (c i) t -> p c t i", i=4),
+                                   y[:, :, c1:c2].rearrange("p t (c i) -> p c t i", i=4))
+                for c0, c1, c2 in pieces:
+                    nc.vector.quantize_mx(codes[:, c0:c2].bitcast(FP8X4), y_s[h][:, g, c0:c2],
+                                          grouped[:, c0:c2, :].rearrange("p j t -> p (j t)"))
+                    planes.append((out_1[g].rearrange("p m t -> p (m t)")[:, 4 * (HALF * h + c0) : 4 * (HALF * h + c2)],
+                                   codes[:, c0:c2]))
             for q in range(4):
-                nc.sync.dma_start(out_2[:, 4 * q : 4 * q + 4, cols].rearrange("g r m -> r g m").bitcast(I32),
-                                  y_s[h][32 * q : 32 * q + 4].bitcast(I32))
+                planes.append((out_2[:, 4 * q : 4 * q + 4, cols].rearrange("g r m -> r g m"), y_s[h][32 * q : 32 * q + 4]))
+        store_planes()

@@ -17,9 +17,18 @@ ACT = mybir.ActivationFunctionType
 ALU = mybir.AluOpType
 
 P = 128
+PASS = 512
 HALF = 512
-Y_VEC = 256
-Y_VEC_LAST = 176
+SLICES = 8
+LAST = SLICES - 1
+Y_VECTOR_COLUMNS = 256
+Y_VECTOR_COLUMNS_LAST = 176
+PAGE_BUFS = 5
+RAW_BUFS = 3
+GROUPED_BUFS = 3
+TANH_BUFS = 3
+SNOW_BUFS = 2
+Z_BANKS = 5
 
 
 def tile_list_glide_slab_page_kernel(
@@ -36,23 +45,23 @@ def tile_list_glide_slab_page_kernel(
         def kept(shape, dtype, name, tag=""):
             return keep.tile(shape, dtype, name=name, tag=tag or name, align_bytes=64)
 
-        def load_list(src, n, name):
-            tile = keep.tile([P, n // 16], U16, name=name)
+        def load_list(src, entries, name):
+            tile = keep.tile([P, entries // 16], U16, name=name)
             nc.sync.dma_start(tile[:], src)
             return tile
 
-        def load_scale_rows(plane, src):
+        def load_scale_rows(tile, src):
             passes = src.shape[0]
             for q in range(4):
-                nc.sync.dma_start(plane[32 * q : 32 * q + 4, :].rearrange("r (a n) -> r a n", a=passes),
+                nc.sync.dma_start(tile[32 * q : 32 * q + 4, :].rearrange("r (a n) -> r a n", a=passes),
                                   src[:, 4 * q : 4 * q + 4, :].rearrange("a r n -> r a n").bitcast(I32))
 
         tab2_s = kept([P, T3 // 4], I32, "tab2_s")
         wf_s_raw = kept([P, H // 4], I32, "wf_s_raw")
         tab_s = kept([P, 2 * T // 4], I32, "tab_s")
         wv_s_raw = kept([P, 2 * H // 4], I32, "wv_s_raw")
-        for plane in [wf_s_raw, tab2_s, tab_s, wv_s_raw]:
-            nc.vector.memset(plane[:], 0)
+        for scale_tile in [wf_s_raw, tab2_s, tab_s, wv_s_raw]:
+            nc.vector.memset(scale_tile[:], 0)
 
         pages = {}
         h2 = {}
@@ -60,12 +69,12 @@ def tile_list_glide_slab_page_kernel(
 
         def load_floor(s):
             b, t = divmod(s, 4)
-            h2[s] = kept([P, S], F32, "floor%d" % s, tag="row%d" % s)
+            h2[s] = kept([P, S], F32, "floor%d" % s)
             nc.sync.dma_start(h2[s][:], floors.rearrange("(b p t) j -> b t p j", b=2, t=4)[b, t])
 
         def load_page(s):
             b, t = divmod(s, 4)
-            pages[s] = ring.tile([P, T2], F32, name="page", bufs=5)
+            pages[s] = ring.tile([P, T2], F32, name="page", bufs=PAGE_BUFS)
             nc.sync.dma_start(pages[s][:], page0.rearrange("(b p t) j -> b t p j", b=2, t=4)[b, t])
 
         def load_gate(src, t0, t1, name):
@@ -74,9 +83,15 @@ def tile_list_glide_slab_page_kernel(
                 nc.sync.dma_start(tile[32 * q : 32 * (q + 1)], src.rearrange("(m t) j -> m t j", t=4)[:, t0:t1, :])
             return [tile[:, t, :] for t in range(t1 - t0)]
 
+        def load_column(src, name):
+            tile = kept([P, 2, 4], F32, name)
+            nc.sync.dma_start(tile[:], src.rearrange("(b p t) -> p b t", b=2, t=4))
+            return tile
+
         def load_weight(w, a, b):
-            raw = ring.tile([P, 4, HALF], F32, name="w_raw", tag="raw", bufs=3, align_bytes=64)
-            nc.sync.dma_start(raw[:], w[512 * a : 512 * (a + 1), 512 * b : 512 * (b + 1)].rearrange("(p i) c -> p i c", i=4))
+            raw = ring.tile([P, 4, PASS], F32, name="w_raw", tag="raw", bufs=RAW_BUFS, align_bytes=64)
+            chunk = w[PASS * a : PASS * (a + 1), PASS * b : PASS * (b + 1)]
+            nc.sync.dma_start(raw[:], chunk.rearrange("(p i) c -> p i c", i=4))
             return raw
 
         def load_table(a):
@@ -85,30 +100,32 @@ def tile_list_glide_slab_page_kernel(
             return tile
 
         def round_columns(grouped, raw, t0, t1):
-            nc.scalar.copy(grouped[:, HALF * t0 : HALF * t1].rearrange("p (t m i) -> p m t i", t=t1 - t0, i=4),
+            nc.scalar.copy(grouped[:, PASS * t0 : PASS * t1].rearrange("p (t m i) -> p m t i", t=t1 - t0, i=4),
                            raw[:].rearrange("p i (m t) -> p m t i", t=4)[:, :, t0:t1, :])
 
         def round_weight(raw):
-            grouped = ring.tile([P, 4 * HALF], BF16, name="w_grouped", tag="grouped", bufs=3, align_bytes=64)
+            grouped = ring.tile([P, 4 * PASS], BF16, name="w_grouped", tag="grouped", bufs=GROUPED_BUFS, align_bytes=64)
             round_columns(grouped, raw, 0, 4)
             return grouped[:]
 
         def quantise_by_slices(raw, name):
-            grouped = ring.tile([P, 4 * HALF], BF16, name="w_grouped", tag="grouped", bufs=3, align_bytes=64)
-            codes = kept([P, HALF], U32, name + "_w")
-            scales = kept([P, HALF], U8, name + "_s")
+            grouped = ring.tile([P, 4 * PASS], BF16, name="w_grouped", tag="grouped", bufs=GROUPED_BUFS, align_bytes=64)
+            codes = kept([P, PASS], U32, name + "_w")
+            scales = kept([P, PASS], U8, name + "_s")
             for t0, t1 in ((0, 1), (1, 2), (2, 4)):
                 round_columns(grouped, raw, t0, t1)
                 nc.vector.quantize_mx(codes[:, P * t0 : P * t1].bitcast(FP8X4), scales[:, P * t0 : P * t1],
-                                      grouped[:, HALF * t0 : HALF * t1])
+                                      grouped[:, PASS * t0 : PASS * t1])
             return codes[:], scales
 
-        def quantise(grouped, name, codes=None):
-            if codes is None:
-                codes = kept([P, HALF], U32, name + "_w")[:]
-            scales = kept([P, HALF], U8, name + "_s")
+        def quantise(grouped, codes, name):
+            scales = kept([P, PASS], U8, name + "_s")
             nc.vector.quantize_mx(codes.bitcast(FP8X4), scales[:], grouped)
             return codes, scales
+
+        def code_tiles(count, name, tag=""):
+            tile = kept([P, count, PASS], U32, name, tag)
+            return [tile[:, c, :] for c in range(count)]
 
         v2_w = kept([P, S], U32, "v2_w")
         v2_s = kept([P, S], U8, "v2_s")
@@ -116,21 +133,67 @@ def tile_list_glide_slab_page_kernel(
         wf_s = kept([P, H], U8, "wf_s")
         wv_w = kept([P, 2 * H], U16, "wv_w")
         wv_s = kept([P, 2 * H], U8, "wv_s")
+        v_w = [kept([P, S], U32, "v_w%d" % a) for a in range(2)]
+        v_s = [kept([P, S], U8, "v_s%d" % a) for a in range(2)]
+        wt_q = {}
+        wo_q = {}
+        x_q = {}
 
         def friction(s):
-            cols = slice(128 * s, 128 * (s + 1))
-            ps = psum.tile([P, S], F32, name="f_ps")
-            nc.tensor.matmul_mx(ps[:], lhsT=wf_w[:, cols].bitcast(FP8X4), lhsT_scale=wf_s[:, cols],
+            cols = slice(P * s, P * (s + 1))
+            f_ps = psum.tile([P, S], F32, name="f_ps")
+            nc.tensor.matmul_mx(f_ps[:], lhsT=wf_w[:, cols].bitcast(FP8X4), lhsT_scale=wf_s[:, cols],
                                 rhs=v2_w[:].bitcast(FP8X4), rhs_scale=v2_s[:], start=True, stop=True)
-            nc.vector.tensor_tensor(h2[s][:], ps[:], h2[s][:], ALU.max)
+            nc.vector.tensor_tensor(h2[s][:], f_ps[:], h2[s][:], ALU.max)
 
         def put_friction(s):
             nc.vector.tensor_tensor(pages[s][:].indirect(l4[:]), h2[s][:], g2[s % 4], ALU.mult)
 
-        wt_q = {}
-        wo_q = {}
-        v_w = [kept([P, S], U32, "v_w%d" % a) for a in range(2)]
-        v_s = [kept([P, S], U8, "v_s%d" % a) for a in range(2)]
+        def snow(s):
+            b, t = divmod(s, 4)
+            a_ps = psum.tile([P, S], F32, name="a_ps")
+            s_ps = psum.tile([P, S], F32, name="s_ps")
+            tcols = slice(P * t, P * (t + 1))
+            for a in range(2):
+                codes, scales = wt_q[a, b]
+                nc.tensor.matmul_mx(a_ps[:], lhsT=codes[:, tcols].bitcast(FP8X4), lhsT_scale=scales[:, tcols],
+                                    rhs=v_w[a][:].bitcast(FP8X4), rhs_scale=v_s[a][:], start=(a == 0), stop=(a == 1))
+            for a in range(2):
+                cols = slice(H * a + P * s, H * a + P * (s + 1))
+                nc.tensor.matmul_mx(s_ps[:], lhsT=wv_w[:, cols].bitcast(FP4X4), lhsT_scale=wv_s[:, cols],
+                                    rhs=v_w[a][:].bitcast(FP8X4), rhs_scale=v_s[a][:], start=(a == 0), stop=(a == 1))
+            th = ring.tile([P, S], F32, name="th", bufs=TANH_BUFS)
+            nc.scalar.activation(th[:], a_ps[:], ACT.Tanh)
+            h1[s] = ring.tile([P, S], F32, name="h1")
+            if s == 0:
+                nc.vector.tensor_tensor(h1[s][:], s_ps[:], th[:], ALU.mult)
+            else:
+                sn = ring.tile([P, S], F32, name="sn", bufs=SNOW_BUFS)
+                nc.scalar.copy(sn[:], s_ps[:])
+                nc.gpsimd.tensor_tensor(h1[s][:], sn[:], th[:], ALU.mult)
+
+        def put_snow(s):
+            nc.vector.tensor_tensor(pages[s][:].indirect(l3[:]), h1[s][:], g1[s % 4], ALU.mult)
+
+        slots = {}
+        x_grouped = {}
+
+        def fetch(s):
+            b, t = divmod(s, 4)
+            for h in range(2):
+                if t == 0:
+                    slots[b, h] = kept([P, 4, HALF], F32, "slots%d%d" % (b, h), tag="tab_w%d" % h if b == 1 else "")
+                    x_grouped[b, h] = kept([P, HALF, 4], BF16, "x_grouped%d%d" % (b, h))
+                width = HALF // 2 if (s, h) == (LAST, 0) else HALF
+                for c0 in range(0, HALF, width):
+                    picked = slots[b, h][:, t, c0 : c0 + width]
+                    entries = l5[:, (HALF * h + c0) // 16 : (HALF * h + c0 + width) // 16]
+                    nc.vector.tensor_copy(picked, pages[s][:].indirect(entries))
+                    nc.scalar.activation(x_grouped[b, h][:, c0 : c0 + width, t], picked, ACT.Identity,
+                                         bias=shift_col[:, b, t : t + 1])
+
+        def quantise_x(b, h, codes):
+            x_q[b, h] = quantise(x_grouped[b, h][:].rearrange("p j t -> p (j t)"), codes, "x%d%d" % (b, h))
 
         l2 = load_list(offs2, S, "l2")
         l4 = load_list(offs4, S, "l4")
@@ -140,7 +203,7 @@ def tile_list_glide_slab_page_kernel(
         tab2_w = kept([P, T3], U32, "tab2_w")
         nc.sync.dma_start(tab2_w[:].bitcast(I32), tab2_words[0].rearrange("p t i -> p (t i)").bitcast(I32))
         nc.vector.tensor_copy(v2_w[:], tab2_w[:].indirect(l2[:]))
-        wf_raw = ring.tile([P, H], I32, name="wf_raw", tag="raw", bufs=3, align_bytes=64)
+        wf_raw = ring.tile([P, H], I32, name="wf_raw", tag="raw", bufs=RAW_BUFS, align_bytes=64)
         nc.sync.dma_start(wf_raw[:], wf_words[0].rearrange("p c i -> p (c i)").bitcast(I32))
         nc.vector.tensor_copy(wf_w[:].rearrange("p (b t m) -> p b m t", b=2, t=4),
                               wf_raw[:].rearrange("p (b m t) -> p b m t", b=2, t=4))
@@ -151,15 +214,17 @@ def tile_list_glide_slab_page_kernel(
         load_page(0)
         g2 = load_gate(wg2, 0, 1, "g2_first")
         put_friction(0)
+
         l1 = load_list(offs, S, "l1")
-        wv_raw = ring.tile([P, 2, H // 2], I32, name="wv_raw", tag="raw", bufs=3, align_bytes=64)
+        wv_raw = ring.tile([P, 2, H // 2], I32, name="wv_raw", tag="raw", bufs=RAW_BUFS, align_bytes=64)
         nc.sync.dma_start(wv_raw[:], wv_words.rearrange("a p c -> p a c").bitcast(I32))
+        wv_raw_words = wv_raw[:].rearrange("p a c -> p (a c)").bitcast(U16)
         nc.vector.tensor_copy(wv_w[:].rearrange("p (c t m) -> p c t m", c=4, t=4),
-                              wv_raw[:].rearrange("p a c -> p (a c)").bitcast(U16).rearrange("p (c m t) -> p c t m", c=4, t=4))
+                              wv_raw_words.rearrange("p (c m t) -> p c t m", c=4, t=4))
         load_scale_rows(wv_s_raw, wv_scales)
         nc.vector.tensor_copy(wv_s[:].rearrange("p (c t m) -> p c t m", c=4, t=4),
                               wv_s_raw[:].bitcast(U8).rearrange("p (c m t) -> p c t m", c=4, t=4))
-        wt_q[0, 0] = quantise(round_weight(load_weight(wt, 0, 0)), "wt00")
+        wt_q[0, 0] = quantise(round_weight(load_weight(wt, 0, 0)), kept([P, PASS], U32, "wt00_w")[:], "wt00")
         nc.vector.tensor_copy(v_w[0][:], load_table(0)[:].indirect(l1[:]))
         load_scale_rows(tab_s, tab_scales)
         for a in range(2):
@@ -171,145 +236,102 @@ def tile_list_glide_slab_page_kernel(
         load_floor(1)
         friction(1)
         l5 = load_list(offs5, NP, "l5")
-        shift_col = kept([P, 2, 4], F32, "shift_col")
-        nc.sync.dma_start(shift_col[:], shift.rearrange("(b p t) -> p b t", b=2, t=4))
-
-        def snow(s):
-            b, t = divmod(s, 4)
-            a_ps = psum.tile([P, S], F32, name="a_ps")
-            s_ps = psum.tile([P, S], F32, name="s_ps")
-            tcols = slice(128 * t, 128 * (t + 1))
-            for a in range(2):
-                codes, scales = wt_q[a, b]
-                nc.tensor.matmul_mx(a_ps[:], lhsT=codes[:, tcols].bitcast(FP8X4), lhsT_scale=scales[:, tcols],
-                                    rhs=v_w[a][:].bitcast(FP8X4), rhs_scale=v_s[a][:], start=(a == 0), stop=(a == 1))
-            for a in range(2):
-                cols = slice(H * a + 128 * s, H * a + 128 * (s + 1))
-                nc.tensor.matmul_mx(s_ps[:], lhsT=wv_w[:, cols].bitcast(FP4X4), lhsT_scale=wv_s[:, cols],
-                                    rhs=v_w[a][:].bitcast(FP8X4), rhs_scale=v_s[a][:], start=(a == 0), stop=(a == 1))
-            th = ring.tile([P, S], F32, name="th", bufs=3)
-            nc.scalar.activation(th[:], a_ps[:], ACT.Tanh)
-            h1[s] = ring.tile([P, S], F32, name="h1")
-            if s == 0:
-                nc.vector.tensor_tensor(h1[s][:], s_ps[:], th[:], ALU.mult)
-            else:
-                sn = ring.tile([P, S], F32, name="sn", bufs=2)
-                nc.scalar.copy(sn[:], s_ps[:])
-                nc.gpsimd.tensor_tensor(h1[s][:], sn[:], th[:], ALU.mult)
-
-        def put_snow(s):
-            nc.vector.tensor_tensor(pages[s][:].indirect(l3[:]), h1[s][:], g1[s % 4], ALU.mult)
-
-        slots = {}
-        x_grouped = {}
-        x_q = {}
-
-        def fetch(s):
-            b, t = divmod(s, 4)
-            for h in range(2):
-                if t == 0:
-                    slots[b, h] = kept([P, 4, HALF], F32, "slots%d%d" % (b, h), tag="tab_w%d" % h if b == 1 else "")
-                    x_grouped[b, h] = kept([P, HALF, 4], BF16, "x_grouped%d%d" % (b, h))
-                nc.vector.tensor_copy(slots[b, h][:, t, :], pages[s][:].indirect(l5[:, 32 * h : 32 * (h + 1)]))
-                nc.scalar.activation(x_grouped[b, h][:, :, t], slots[b, h][:, t, :], ACT.Identity,
-                                     bias=shift_col[:, b, t : t + 1])
-
-        def x_rows(b, h):
-            return x_grouped[b, h][:].rearrange("p j t -> p (j t)")
-
-        def after_floor(s, count, name):
-            return kept([P, count, HALF], U32, name, tag="row%d" % s)
-
+        shift_col = load_column(shift, "shift_col")
         snow(0)
         put_snow(0)
         snow(1)
         fetch(0)
         g2 = g2 + load_gate(wg2, 1, 4, "g2_rest")
-        late_rows = []
-        for s in range(1, 8):
-            if 1 < s < 7:
-                a, b = divmod(s - 3, 2)
-                rows = round_weight(load_weight(wt, 1, 1) if s == 2 else load_weight(wo, b, a))
+
+        chunks = [(wt, 0, 1), (wt, 1, 1), (wo, 0, 0), (wo, 1, 0), (wo, 0, 1), (wo, 1, 1)]
+        rounded = {}
+        for s in range(1, SLICES):
+            if 1 < s < LAST:
+                rounded[s] = round_weight(load_weight(*chunks[s - 1]))
             load_page(s)
             put_friction(s)
-            if s < 7:
+            if s < LAST:
                 load_floor(s + 1)
                 friction(s + 1)
             if s == 1:
                 g1 = g1 + load_gate(wg1, 1, 4, "g1_rest")
-                gy_col = kept([P, 2, 4], F32, "gy_col")
-                nc.sync.dma_start(gy_col[:], gy.rearrange("(b p t) -> p b t", b=2, t=4))
+                gy_col = load_column(gy, "gy_col")
             put_snow(s)
-            if s < 7:
+            if s < LAST:
                 snow(s + 1)
             if s == 2:
-                codes = after_floor(s, 2, "wt_1_w")
-                wt_q[0, 1] = quantise(wt01_rows, "wt01", codes[:, 0, :])
+                wt_codes = code_tiles(2, "wt_b1_w", "floor2")
+                wt_q[0, 1] = quantise(rounded[1], wt_codes[0], "wt01")
             elif s in (3, 4):
-                wo_q[s - 3, 0] = quantise(rows, "wo%d0" % (s - 3), after_floor(s, 1, "wo%d0_w" % (s - 3))[:, 0, :])
-            elif s in (5, 6):
-                late_rows.append(rows)
-            if s == 5:
-                x_q[0, 0] = quantise(x_rows(0, 0), "x00", after_floor(s, 1, "x00_w")[:, 0, :])
+                a = s - 3
+                wo_q[a, 0] = quantise(rounded[s], code_tiles(1, "wo%d0_w" % a, "floor%d" % s)[0], "wo%d0" % a)
+            elif s == 5:
+                quantise_x(0, 0, code_tiles(1, "x00_w", "floor5")[0])
             fetch(s)
             if s == 1:
-                wt01_rows = round_weight(load_weight(wt, 0, 1))
+                rounded[s] = round_weight(load_weight(*chunks[0]))
             elif s == 2:
-                wt_q[1, 1] = quantise(rows, "wt11", codes[:, 1, :])
+                wt_q[1, 1] = quantise(rounded[2], wt_codes[1], "wt11")
 
-        late_codes = kept([P, 3, HALF], U32, "late_codes", tag="g1_rest")
-        x_q[1, 0] = quantise(x_rows(1, 0), "x10")
-        for a in range(2):
-            wo_q[a, 1] = quantise(late_rows[a], "wo%d1" % a, late_codes[:, a, :])
-        x_q[0, 1] = quantise(x_rows(0, 1), "x01", late_codes[:, 2, :])
-        x_q[1, 1] = quantise(x_rows(1, 1), "x11")
+        wo_q[0, 1] = quantise(rounded[5], kept([P, PASS], U32, "wo01_w", tag="g1_rest")[:], "wo01")
+        quantise_x(1, 0, kept([P, PASS], U32, "x10_w")[:])
+        late_codes = code_tiles(3, "late_codes", "x_grouped10")
+        wo_q[1, 1] = quantise(rounded[6], late_codes[0], "wo11")
+        quantise_x(0, 1, late_codes[1])
+        quantise_x(1, 1, late_codes[2])
 
         y_s = [kept([P, 2, HALF], U8, "y_s%d" % h) for h in range(2)]
 
-        def z_pass(ps, g, t, h, b):
+        def z_pass(bank, g, t, h, b):
             codes, scales = wo_q[b, g]
-            tcols = slice(128 * t, 128 * (t + 1))
-            nc.tensor.matmul_mx(ps[:], lhsT=codes[:, tcols].bitcast(FP8X4), lhsT_scale=scales[:, tcols],
+            tcols = slice(P * t, P * (t + 1))
+            nc.tensor.matmul_mx(bank[:], lhsT=codes[:, tcols].bitcast(FP8X4), lhsT_scale=scales[:, tcols],
                                 rhs=x_q[b, h][0].bitcast(FP8X4), rhs_scale=x_q[b, h][1][:],
                                 start=(b == 0), stop=(b == 1))
 
-        planes = []
+        byte_stores = []
 
-        def store_planes():
-            for dst, src in planes:
+        def store_bytes():
+            for dst, src in byte_stores:
                 nc.sync.dma_start(dst.bitcast(I32), src.bitcast(I32))
-            planes.clear()
+            byte_stores.clear()
 
         for h in range(2):
             cols = slice(HALF * h, HALF * (h + 1))
             for g in range(2):
-                last = h == 1 and g == 1
                 y = slots[g, h]
-                y_rows = out_0[512 * g : 512 * (g + 1), cols].rearrange("(p t) j -> p t j", t=4)
-                banks = [psum.tile([P, HALF], F32, name="z_ps", bufs=5) for t in range(4)]
+                y_rows = out_0[PASS * g : PASS * (g + 1), cols].rearrange("(p t) j -> p t j", t=4)
+                banks = [psum.tile([P, HALF], F32, name="z_ps", bufs=Z_BANKS) for t in range(4)]
                 for t in range(4):
                     z_pass(banks[t], g, t, h, 0)
                 for t in range(4):
                     z_pass(banks[t], g, t, h, 1)
-                    tz = ring.tile([P, HALF], F32, name="tz", bufs=3)
+                    tz = ring.tile([P, HALF], F32, name="tz", bufs=TANH_BUFS)
                     nc.scalar.activation(tz[:], banks[t][:], ACT.Tanh)
-                    nc.vector.scalar_tensor_tensor(y[:, t, :], y[:, t, :], gy_col[:, g, t : t + 1], tz[:], ALU.mult, ALU.add)
+                    nc.vector.scalar_tensor_tensor(y[:, t, :], y[:, t, :], gy_col[:, g, t : t + 1], tz[:],
+                                                   ALU.mult, ALU.add)
                     nc.sync.dma_start(y_rows[:, t, :], y[:, t, :])
                     if t == 1:
-                        store_planes()
-                grouped = ring.tile([P, HALF, 4], BF16, name="y_grouped", tag="grouped", bufs=3, align_bytes=64)
+                        store_bytes()
+
+                grouped = ring.tile([P, HALF, 4], BF16, name="y_grouped", tag="grouped", bufs=GROUPED_BUFS,
+                                    align_bytes=64)
                 codes = kept([P, HALF], U32, "y%d%d_w" % (g, h))
-                pieces = [(0, Y_VEC_LAST, 256), (256, 256 + Y_VEC_LAST, HALF)] if last else [(0, Y_VEC, HALF)]
+                if (h, g) == (1, 1):
+                    pieces = [(c0, c0 + Y_VECTOR_COLUMNS_LAST, c0 + HALF // 2) for c0 in (0, HALF // 2)]
+                else:
+                    pieces = [(0, Y_VECTOR_COLUMNS, HALF)]
                 for c0, c1, c2 in pieces:
                     nc.vector.tensor_copy(grouped[:, c0:c1, :].rearrange("p (c i) t -> p c t i", i=4),
                                           y[:, :, c0:c1].rearrange("p t (c i) -> p c t i", i=4))
                     nc.scalar.copy(grouped[:, c1:c2, :].rearrange("p (c i) t -> p c t i", i=4),
                                    y[:, :, c1:c2].rearrange("p t (c i) -> p c t i", i=4))
+                out_words = out_1[g].rearrange("p m t -> p (m t)")
                 for c0, c1, c2 in pieces:
                     nc.vector.quantize_mx(codes[:, c0:c2].bitcast(FP8X4), y_s[h][:, g, c0:c2],
                                           grouped[:, c0:c2, :].rearrange("p j t -> p (j t)"))
-                    planes.append((out_1[g].rearrange("p m t -> p (m t)")[:, 4 * (HALF * h + c0) : 4 * (HALF * h + c2)],
-                                   codes[:, c0:c2]))
+                    byte_stores.append((out_words[:, 4 * (HALF * h + c0) : 4 * (HALF * h + c2)], codes[:, c0:c2]))
             for q in range(4):
-                planes.append((out_2[:, 4 * q : 4 * q + 4, cols].rearrange("g r m -> r g m"), y_s[h][32 * q : 32 * q + 4]))
-        store_planes()
+                byte_stores.append((out_2[:, 4 * q : 4 * q + 4, cols].rearrange("g r m -> r g m"),
+                                    y_s[h][32 * q : 32 * q + 4]))
+        store_bytes()

from contextlib import ExitStack

import concourse.mybir as mybir

K, K2, H, T, T3, S, T2, NP = 1024, 512, 1024, 2048, 1024, 512, 2048, 1024
FLOPS = 2 * (2 * K * H * S + K2 * H * S + H * H * NP)

F32 = mybir.dt.float32
BF16 = mybir.dt.bfloat16
I32 = mybir.dt.int32
U32 = mybir.dt.uint32
U16 = mybir.dt.uint16
U8 = mybir.dt.uint8
FP8X4 = mybir.dt.float8_e4m3fn_x4
FP4X4 = mybir.dt.float4_e2m1fn_x4
ACT = mybir.ActivationFunctionType
ALU = mybir.AluOpType

P = 128
PASS = 512
HALF = 512
SLICES = 8
LAST = SLICES - 1
Y_VECTOR_COLUMNS = 256
Y_VECTOR_COLUMNS_LAST = 176
PAGE_BUFS = 5
RAW_BUFS = 3
GROUPED_BUFS = 3
TANH_BUFS = 3
SNOW_BUFS = 2
Z_BANKS = 5


def tile_list_glide_slab_page_kernel(
    tc, tab_words, tab_scales, tab2_words, tab2_scales, offs, offs2, offs3, offs4, offs5,
    wt, wv_words, wv_scales, wf_words, wf_scales, floors, wg1, wg2, page0, shift, wo, gy,
    out_0, out_1, out_2,
):
    nc = tc.nc
    with ExitStack() as ctx:
        keep = ctx.enter_context(tc.tile_pool(name="keep", bufs=1))
        ring = ctx.enter_context(tc.tile_pool(name="ring", bufs=1))
        psum = ctx.enter_context(tc.psum_pool(name="psum", bufs=1))

        def kept(shape, dtype, name, tag=""):
            return keep.tile(shape, dtype, name=name, tag=tag or name, align_bytes=64)

        def load_list(src, entries, name):
            tile = keep.tile([P, entries // 16], U16, name=name)
            nc.sync.dma_start(tile[:], src)
            return tile

        def load_scale_rows(tile, src):
            passes = src.shape[0]
            for q in range(4):
                nc.sync.dma_start(tile[32 * q : 32 * q + 4, :].rearrange("r (a n) -> r a n", a=passes),
                                  src[:, 4 * q : 4 * q + 4, :].rearrange("a r n -> r a n").bitcast(I32))

        tab2_s = kept([P, T3 // 4], I32, "tab2_s")
        wf_s_raw = kept([P, H // 4], I32, "wf_s_raw")
        tab_s = kept([P, 2 * T // 4], I32, "tab_s")
        wv_s_raw = kept([P, 2 * H // 4], I32, "wv_s_raw")
        for scale_tile in [wf_s_raw, tab2_s, tab_s, wv_s_raw]:
            nc.vector.memset(scale_tile[:], 0)

        pages = {}
        h2 = {}
        h1 = {}

        def load_floor(s):
            b, t = divmod(s, 4)
            h2[s] = kept([P, S], F32, "floor%d" % s)
            nc.sync.dma_start(h2[s][:], floors.rearrange("(b p t) j -> b t p j", b=2, t=4)[b, t])

        def load_page(s):
            b, t = divmod(s, 4)
            pages[s] = ring.tile([P, T2], F32, name="page", bufs=PAGE_BUFS)
            nc.sync.dma_start(pages[s][:], page0.rearrange("(b p t) j -> b t p j", b=2, t=4)[b, t])

        def load_gate(src, t0, t1, name):
            tile = kept([P, t1 - t0, S], F32, name)
            for q in range(4):
                nc.sync.dma_start(tile[32 * q : 32 * (q + 1)], src.rearrange("(m t) j -> m t j", t=4)[:, t0:t1, :])
            return [tile[:, t, :] for t in range(t1 - t0)]

        def load_column(src, name):
            tile = kept([P, 2, 4], F32, name)
            nc.sync.dma_start(tile[:], src.rearrange("(b p t) -> p b t", b=2, t=4))
            return tile

        def load_weight(w, a, b):
            raw = ring.tile([P, 4, PASS], F32, name="w_raw", tag="raw", bufs=RAW_BUFS, align_bytes=64)
            chunk = w[PASS * a : PASS * (a + 1), PASS * b : PASS * (b + 1)]
            nc.sync.dma_start(raw[:], chunk.rearrange("(p i) c -> p i c", i=4))
            return raw

        def load_table(a):
            tile = kept([P, T], U32, "tab_w%d" % a)
            nc.sync.dma_start(tile[:].bitcast(I32), tab_words[a].rearrange("p t i -> p (t i)").bitcast(I32))
            return tile

        def round_columns(grouped, raw, t0, t1):
            nc.scalar.copy(grouped[:, PASS * t0 : PASS * t1].rearrange("p (t m i) -> p m t i", t=t1 - t0, i=4),
                           raw[:].rearrange("p i (m t) -> p m t i", t=4)[:, :, t0:t1, :])

        def round_weight(raw):
            grouped = ring.tile([P, 4 * PASS], BF16, name="w_grouped", tag="grouped", bufs=GROUPED_BUFS, align_bytes=64)
            round_columns(grouped, raw, 0, 4)
            return grouped[:]

        def quantise_by_slices(raw, name):
            grouped = ring.tile([P, 4 * PASS], BF16, name="w_grouped", tag="grouped", bufs=GROUPED_BUFS, align_bytes=64)
            codes = kept([P, PASS], U32, name + "_w")
            scales = kept([P, PASS], U8, name + "_s")
            for t0, t1 in ((0, 1), (1, 2), (2, 4)):
                round_columns(grouped, raw, t0, t1)
                nc.vector.quantize_mx(codes[:, P * t0 : P * t1].bitcast(FP8X4), scales[:, P * t0 : P * t1],
                                      grouped[:, PASS * t0 : PASS * t1])
            return codes[:], scales

        def quantise(grouped, codes, name):
            scales = kept([P, PASS], U8, name + "_s")
            nc.vector.quantize_mx(codes.bitcast(FP8X4), scales[:], grouped)
            return codes, scales

        def code_tiles(count, name, tag=""):
            tile = kept([P, count, PASS], U32, name, tag)
            return [tile[:, c, :] for c in range(count)]

        v2_w = kept([P, S], U32, "v2_w")
        v2_s = kept([P, S], U8, "v2_s")
        wf_w = kept([P, H], I32, "wf_w")
        wf_s = kept([P, H], U8, "wf_s")
        wv_w = kept([P, 2 * H], U16, "wv_w")
        wv_s = kept([P, 2 * H], U8, "wv_s")
        v_w = [kept([P, S], U32, "v_w%d" % a) for a in range(2)]
        v_s = [kept([P, S], U8, "v_s%d" % a) for a in range(2)]
        wt_q = {}
        wo_q = {}
        x_q = {}

        def friction(s):
            cols = slice(P * s, P * (s + 1))
            f_ps = psum.tile([P, S], F32, name="f_ps")
            nc.tensor.matmul_mx(f_ps[:], lhsT=wf_w[:, cols].bitcast(FP8X4), lhsT_scale=wf_s[:, cols],
                                rhs=v2_w[:].bitcast(FP8X4), rhs_scale=v2_s[:], start=True, stop=True)
            nc.vector.tensor_tensor(h2[s][:], f_ps[:], h2[s][:], ALU.max)

        def put_friction(s):
            nc.vector.tensor_tensor(pages[s][:].indirect(l4[:]), h2[s][:], g2[s % 4], ALU.mult)

        def snow(s):
            b, t = divmod(s, 4)
            a_ps = psum.tile([P, S], F32, name="a_ps")
            s_ps = psum.tile([P, S], F32, name="s_ps")
            tcols = slice(P * t, P * (t + 1))
            for a in range(2):
                codes, scales = wt_q[a, b]
                nc.tensor.matmul_mx(a_ps[:], lhsT=codes[:, tcols].bitcast(FP8X4), lhsT_scale=scales[:, tcols],
                                    rhs=v_w[a][:].bitcast(FP8X4), rhs_scale=v_s[a][:], start=(a == 0), stop=(a == 1))
            for a in range(2):
                cols = slice(H * a + P * s, H * a + P * (s + 1))
                nc.tensor.matmul_mx(s_ps[:], lhsT=wv_w[:, cols].bitcast(FP4X4), lhsT_scale=wv_s[:, cols],
                                    rhs=v_w[a][:].bitcast(FP8X4), rhs_scale=v_s[a][:], start=(a == 0), stop=(a == 1))
            th = ring.tile([P, S], F32, name="th", bufs=TANH_BUFS)
            nc.scalar.activation(th[:], a_ps[:], ACT.Tanh)
            h1[s] = ring.tile([P, S], F32, name="h1")
            if s == 0:
                nc.vector.tensor_tensor(h1[s][:], s_ps[:], th[:], ALU.mult)
            else:
                sn = ring.tile([P, S], F32, name="sn", bufs=SNOW_BUFS)
                nc.scalar.copy(sn[:], s_ps[:])
                nc.gpsimd.tensor_tensor(h1[s][:], sn[:], th[:], ALU.mult)

        def put_snow(s):
            nc.vector.tensor_tensor(pages[s][:].indirect(l3[:]), h1[s][:], g1[s % 4], ALU.mult)

        slots = {}
        x_grouped = {}

        def fetch(s):
            b, t = divmod(s, 4)
            for h in range(2):
                if t == 0:
                    slots[b, h] = kept([P, 4, HALF], F32, "slots%d%d" % (b, h), tag="tab_w%d" % h if b == 1 else "")
                    x_grouped[b, h] = kept([P, HALF, 4], BF16, "x_grouped%d%d" % (b, h))
                width = HALF // 2 if (s, h) == (LAST, 0) else HALF
                for c0 in range(0, HALF, width):
                    picked = slots[b, h][:, t, c0 : c0 + width]
                    entries = l5[:, (HALF * h + c0) // 16 : (HALF * h + c0 + width) // 16]
                    nc.vector.tensor_copy(picked, pages[s][:].indirect(entries))
                    nc.scalar.activation(x_grouped[b, h][:, c0 : c0 + width, t], picked, ACT.Identity,
                                         bias=shift_col[:, b, t : t + 1])

        def quantise_x(b, h, codes):
            x_q[b, h] = quantise(x_grouped[b, h][:].rearrange("p j t -> p (j t)"), codes, "x%d%d" % (b, h))

        l2 = load_list(offs2, S, "l2")
        l4 = load_list(offs4, S, "l4")
        load_scale_rows(wf_s_raw, wf_scales)
        nc.vector.tensor_copy(wf_s[:].rearrange("p (b t m) -> p b t m", b=2, t=4),
                              wf_s_raw[:].bitcast(U8).rearrange("p (b m t) -> p b t m", b=2, t=4))
        tab2_w = kept([P, T3], U32, "tab2_w")
        nc.sync.dma_start(tab2_w[:].bitcast(I32), tab2_words[0].rearrange("p t i -> p (t i)").bitcast(I32))
        nc.vector.tensor_copy(v2_w[:], tab2_w[:].indirect(l2[:]))
        wf_raw = ring.tile([P, H], I32, name="wf_raw", tag="raw", bufs=RAW_BUFS, align_bytes=64)
        nc.sync.dma_start(wf_raw[:], wf_words[0].rearrange("p c i -> p (c i)").bitcast(I32))
        nc.vector.tensor_copy(wf_w[:].rearrange("p (b t m) -> p b m t", b=2, t=4),
                              wf_raw[:].rearrange("p (b m t) -> p b m t", b=2, t=4))
        load_scale_rows(tab2_s, tab2_scales)
        nc.vector.tensor_copy(v2_s[:], tab2_s[:].bitcast(U8).indirect(l2[:]))
        load_floor(0)
        friction(0)
        load_page(0)
        g2 = load_gate(wg2, 0, 1, "g2_first")
        put_friction(0)

        l1 = load_list(offs, S, "l1")
        wv_raw = ring.tile([P, 2, H // 2], I32, name="wv_raw", tag="raw", bufs=RAW_BUFS, align_bytes=64)
        nc.sync.dma_start(wv_raw[:], wv_words.rearrange("a p c -> p a c").bitcast(I32))
        wv_raw_words = wv_raw[:].rearrange("p a c -> p (a c)").bitcast(U16)
        nc.vector.tensor_copy(wv_w[:].rearrange("p (c t m) -> p c t m", c=4, t=4),
                              wv_raw_words.rearrange("p (c m t) -> p c t m", c=4, t=4))
        load_scale_rows(wv_s_raw, wv_scales)
        nc.vector.tensor_copy(wv_s[:].rearrange("p (c t m) -> p c t m", c=4, t=4),
                              wv_s_raw[:].bitcast(U8).rearrange("p (c m t) -> p c t m", c=4, t=4))
        wt_q[0, 0] = quantise(round_weight(load_weight(wt, 0, 0)), kept([P, PASS], U32, "wt00_w")[:], "wt00")
        nc.vector.tensor_copy(v_w[0][:], load_table(0)[:].indirect(l1[:]))
        load_scale_rows(tab_s, tab_scales)
        for a in range(2):
            nc.vector.tensor_copy(v_s[a][:], tab_s[:].bitcast(U8)[:, T * a : T * (a + 1)].indirect(l1[:]))
        nc.vector.tensor_copy(v_w[1][:], load_table(1)[:].indirect(l1[:]))
        wt_q[1, 0] = quantise_by_slices(load_weight(wt, 1, 0), "wt10")
        l3 = load_list(offs3, S, "l3")
        g1 = load_gate(wg1, 0, 1, "g1_first")
        load_floor(1)
        friction(1)
        l5 = load_list(offs5, NP, "l5")
        shift_col = load_column(shift, "shift_col")
        snow(0)
        put_snow(0)
        snow(1)
        fetch(0)
        g2 = g2 + load_gate(wg2, 1, 4, "g2_rest")

        chunks = [(wt, 0, 1), (wt, 1, 1), (wo, 0, 0), (wo, 1, 0), (wo, 0, 1), (wo, 1, 1)]
        rounded = {}
        for s in range(1, SLICES):
            if 1 < s < LAST:
                rounded[s] = round_weight(load_weight(*chunks[s - 1]))
            load_page(s)
            put_friction(s)
            if s < LAST:
                load_floor(s + 1)
                friction(s + 1)
            if s == 1:
                g1 = g1 + load_gate(wg1, 1, 4, "g1_rest")
                gy_col = load_column(gy, "gy_col")
            put_snow(s)
            if s < LAST:
                snow(s + 1)
            if s == 2:
                wt_codes = code_tiles(2, "wt_b1_w", "floor2")
                wt_q[0, 1] = quantise(rounded[1], wt_codes[0], "wt01")
            elif s in (3, 4):
                a = s - 3
                wo_q[a, 0] = quantise(rounded[s], code_tiles(1, "wo%d0_w" % a, "floor%d" % s)[0], "wo%d0" % a)
            elif s == 5:
                quantise_x(0, 0, code_tiles(1, "x00_w", "floor5")[0])
            fetch(s)
            if s == 1:
                rounded[s] = round_weight(load_weight(*chunks[0]))
            elif s == 2:
                wt_q[1, 1] = quantise(rounded[2], wt_codes[1], "wt11")

        wo_q[0, 1] = quantise(rounded[5], kept([P, PASS], U32, "wo01_w", tag="g1_rest")[:], "wo01")
        quantise_x(1, 0, kept([P, PASS], U32, "x10_w")[:])
        late_codes = code_tiles(3, "late_codes", "x_grouped10")
        wo_q[1, 1] = quantise(rounded[6], late_codes[0], "wo11")
        quantise_x(0, 1, late_codes[1])
        quantise_x(1, 1, late_codes[2])

        y_s = [kept([P, 2, HALF], U8, "y_s%d" % h) for h in range(2)]

        def z_pass(bank, g, t, h, b):
            codes, scales = wo_q[b, g]
            tcols = slice(P * t, P * (t + 1))
            nc.tensor.matmul_mx(bank[:], lhsT=codes[:, tcols].bitcast(FP8X4), lhsT_scale=scales[:, tcols],
                                rhs=x_q[b, h][0].bitcast(FP8X4), rhs_scale=x_q[b, h][1][:],
                                start=(b == 0), stop=(b == 1))

        byte_stores = []

        def store_bytes():
            for dst, src in byte_stores:
                nc.sync.dma_start(dst.bitcast(I32), src.bitcast(I32))
            byte_stores.clear()

        for h in range(2):
            cols = slice(HALF * h, HALF * (h + 1))
            for g in range(2):
                y = slots[g, h]
                y_rows = out_0[PASS * g : PASS * (g + 1), cols].rearrange("(p t) j -> p t j", t=4)
                banks = [psum.tile([P, HALF], F32, name="z_ps", bufs=Z_BANKS) for t in range(4)]
                for t in range(4):
                    z_pass(banks[t], g, t, h, 0)
                for t in range(4):
                    z_pass(banks[t], g, t, h, 1)
                    tz = ring.tile([P, HALF], F32, name="tz", bufs=TANH_BUFS)
                    nc.scalar.activation(tz[:], banks[t][:], ACT.Tanh)
                    nc.vector.scalar_tensor_tensor(y[:, t, :], y[:, t, :], gy_col[:, g, t : t + 1], tz[:],
                                                   ALU.mult, ALU.add)
                    nc.sync.dma_start(y_rows[:, t, :], y[:, t, :])
                    if t == 1:
                        store_bytes()

                grouped = ring.tile([P, HALF, 4], BF16, name="y_grouped", tag="grouped", bufs=GROUPED_BUFS,
                                    align_bytes=64)
                codes = kept([P, HALF], U32, "y%d%d_w" % (g, h))
                if (h, g) == (1, 1):
                    pieces = [(c0, c0 + Y_VECTOR_COLUMNS_LAST, c0 + HALF // 2) for c0 in (0, HALF // 2)]
                else:
                    pieces = [(0, Y_VECTOR_COLUMNS, HALF)]
                for c0, c1, c2 in pieces:
                    nc.vector.tensor_copy(grouped[:, c0:c1, :].rearrange("p (c i) t -> p c t i", i=4),
                                          y[:, :, c0:c1].rearrange("p t (c i) -> p c t i", i=4))
                    nc.scalar.copy(grouped[:, c1:c2, :].rearrange("p (c i) t -> p c t i", i=4),
                                   y[:, :, c1:c2].rearrange("p t (c i) -> p c t i", i=4))
                out_words = out_1[g].rearrange("p m t -> p (m t)")
                for c0, c1, c2 in pieces:
                    nc.vector.quantize_mx(codes[:, c0:c2].bitcast(FP8X4), y_s[h][:, g, c0:c2],
                                          grouped[:, c0:c2, :].rearrange("p j t -> p (j t)"))
                    byte_stores.append((out_words[:, 4 * (HALF * h + c0) : 4 * (HALF * h + c2)], codes[:, c0:c2]))
            for q in range(4):
                byte_stores.append((out_2[:, 4 * q : 4 * q + 4, cols].rearrange("g r m -> r g m"),
                                    y_s[h][32 * q : 32 * q + 4]))
        store_bytes()
